import numpy as np, ml_dtypes
CORES = [25,29,65,69,153,157,193,197]
N = 8
import mx_ref
BF = ml_dtypes.bfloat16
def entries(a):
    return np.ascontiguousarray(a.T).reshape(-1)
def table(e):
    return np.ascontiguousarray(np.reshape(e, (-1, 16)).T).astype(np.int32)
def cols(t, e):
    v = np.concatenate([t.reshape(128, -1, 4), np.zeros((128, 1, 4), BF)], axis=1)
    return np.ascontiguousarray(v[:, e]).reshape(128, -1)
def tile(rs):
    return np.stack(rs, axis=2).reshape(128, -1).astype(BF)
def cut(t, i, w=512):
    return t[:, w * i:w * i + w]
def f(rng, *shape):
    return mx_ref.flush((rng.standard_normal(shape, dtype=np.float32) * np.exp2(rng.integers(-2, 3, shape[:-1] + (1,)))).astype(BF))
def wide(rng, *shape, cols=0):
    v = rng.standard_normal(shape, dtype=np.float32) * np.exp2(rng.integers(-12, 13, shape)).astype(np.float32)
    if cols: v *= np.repeat(np.exp2(rng.integers(-cols, cols + 1, shape[:-2] + (1, shape[-1] // 4))) * (rng.random(shape[:-2] + (1, shape[-1] // 4)) > 0.0625), 4, axis=-1).astype(np.float32)
    return mx_ref.flush(v.astype(BF))
T, CAPA, CAPB, TR = 512, 112, 96, 16
def mix(rng, n, la=0, lb=0):
    n = n.copy()
    for _ in range(4000):
        p, q = rng.integers(0, N, (2, 3)); k = rng.integers(0, 4)
        p2, q2 = p.copy(), q.copy(); m = n.copy()
        if k == 3: p2[1] = q[1]
        else: p2[k], q2[k] = q[k], p[k]
        m[tuple(p)] -= 1; m[tuple(p2)] += 1
        if k < 3: m[tuple(q)] -= 1; m[tuple(q2)] += 1
        sa, ab = m.sum(axis=2), m.sum(axis=0)
        if m.min() >= 0 and m.max() <= TR and (sa <= CAPA).all() and (sa >= la).all() and (ab <= CAPB).all() and (ab >= lb).all(): n = m
    return n
def even():
    return np.full((N, N, N), T // N ** 2)
def places(rng, k, cap, by=None):
    out = np.zeros(len(k), int)
    for g in np.unique(k):
        j = np.flatnonzero(k == g)
        if by is None: out[j] = g * cap + rng.permutation(cap)[:len(j)]
        else: out[j[np.argsort(by[j])]] = g * cap + cap - 1 - np.arange(len(j))
    return out
def lists(rng, n, back=False):
    s, a, b = np.repeat(np.argwhere(n >= 0), n.reshape(-1), axis=0).T
    col = np.concatenate([rng.permutation(T) for r in range(N)])
    snd, pas, tri = np.full(N * N * CAPA, -1), np.full(N * N * CAPB, -1), np.full(N * N * N * TR, -1)
    p1 = places(rng, s * N + a, CAPA, col if back else None); snd[p1] = col
    arr = s * CAPA + p1 % CAPA
    p2 = places(rng, a * N + b, CAPB, arr if back else None); pas[p2] = arr
    p3 = places(rng, (s * N + a) * N + b, TR, col if back else None); tri[p3] = col
    c, t = a * CAPB + p2 % CAPB, (s * N + a) * TR + p3 % TR
    plc, plt = [], []
    for r in range(N):
        j = rng.permutation(np.flatnonzero(b == r))
        if back: j = j[np.argsort(-c[j])]
        plc.append(table(c[j])); plt.append(table(t[j]))
    return {"snd": np.stack([table(v) for v in snd.reshape(N, -1)]), "pas": np.stack([table(v) for v in pas.reshape(N, -1)]), "tri": np.stack([table(v) for v in tri.reshape(N, -1)]), "plc": np.stack(plc), "plt": np.stack(plt)}
def values(rng):
    return {"x": f(rng, N, 128, 4 * T), "w": f(rng, N, 128, 2048), "vv": f(rng, N, 128, 512)}
def setup_inputs(rng):
    return {**values(rng), **lists(rng, mix(rng, even()))}
def heavy(rng, d):
    n = even()
    for k in range(CAPB // N - T // N ** 2):
        for s in range(N):
            for a in range(N):
                n[s, a, (a + d) % N] += 1; n[s, a, (a + d + 1 + (s + k) % (N - 1)) % N] -= 1
    return {**values(rng), **lists(rng, mix(rng, n, lb=CAPB * np.roll(np.eye(N, dtype=int), d, axis=1)))}
def setup_inputs_diag(rng):
    return heavy(rng, 0)
def setup_inputs_onward(rng):
    return heavy(rng, int(rng.integers(1, N)))
def setup_inputs_full(rng):
    k = T // CAPA
    g = np.zeros((N, N), int); g[:, :k] = CAPA; g[:, k] = T - k * CAPA
    g = np.stack([np.roll(g[s], s) for s in range(N)])[rng.permutation(N)][:, rng.permutation(N)]
    return {**values(rng), **lists(rng, mix(rng, np.repeat(g[:, :, None] // N, N, axis=2), la=np.where(g == CAPA, CAPA, 0)))}
def setup_inputs_reversed(rng):
    return {**values(rng), **lists(rng, mix(rng, even()), back=True)}
def setup_inputs_spread(rng):
    d = setup_inputs(rng); d["x"] = wide(rng, N, 128, 4 * T); return d
def check_inputs(d):
    b = []
    snd, pas, tri, plc, plt = [[entries(d[k][r]) for r in range(N)] for k in ("snd", "pas", "tri", "plc", "plt")]
    for r in range(N):
        if snd[r].min() < -1 or not np.array_equal(np.sort(snd[r][snd[r] >= 0]), np.arange(T)): b.append("snd")
        if tri[r].min() < -1 or not np.array_equal(np.sort(tri[r][tri[r] >= 0]), np.arange(T)): b.append("tri")
        for a in range(N):
            u, v = snd[r][a * CAPA:(a + 1) * CAPA], tri[r][a * N * TR:(a + 1) * N * TR]
            if not np.array_equal(np.sort(u[u >= 0]), np.sort(v[v >= 0])): b.append("tri")
    arrived = [np.concatenate([snd[s][a * CAPA:(a + 1) * CAPA] for s in range(N)]) for a in range(N)]
    for a in range(N):
        if pas[a].min() < -1 or not np.array_equal(np.sort(pas[a][pas[a] >= 0]), np.flatnonzero(arrived[a] >= 0)): b.append("pas")
    if b: return b
    for r in range(N):
        k = np.concatenate([pas[a][r * CAPB:(r + 1) * CAPB] for a in range(N)])
        t = np.concatenate([tri[s][(a * N + r) * TR:(a * N + r + 1) * TR] for s in range(N) for a in range(N)])
        if not np.array_equal(np.sort(plc[r]), np.flatnonzero(k >= 0)): b.append("plc"); continue
        if not np.array_equal(np.sort(plt[r]), np.flatnonzero(t >= 0)): b.append("plt"); continue
        a, m = plc[r] // CAPB, k[plc[r]]
        if (plt[r] // TR != m // CAPA * N + a).any() or (t[plt[r]] != np.stack(arrived)[a, m]).any(): b.append("plt")
    return b
def reference(x, w, vv, snd, pas, tri, plc, plt):
    h = []
    for a in range(N):
        q = mx_ref.quantize(np.concatenate([cols(x[s], entries(snd[s])[a * CAPA:(a + 1) * CAPA]) for s in range(N)], axis=1))
        h.append(tile([np.maximum(mx_ref.matmul(mx_ref.quantize(cut(w[a], i)), q), np.float32(0)) * np.float32(0.043) for i in range(4)]))
    y = np.zeros((N, 128, T), np.float32)
    for b in range(N):
        t = np.concatenate([cols(h[a], entries(pas[a])[b * CAPB:(b + 1) * CAPB]) for a in range(N)], axis=1)
        y[b] = mx_ref.matmul(mx_ref.quantize(vv[b]), mx_ref.quantize(cols(t, entries(plc[b]))))
    return {"y": y}

@@ -1,0 +1,297 @@
+from concourse.bass import DstId, RemoteDMATransfer
+from concourse.mybir import dt, AluOpType, ActivationFunctionType
+
+Q8 = "float8_e4m3fn_x4"
+SCRATCH = {
+    "trs": ("sbuf", [128, 2, 2, 4, 4], "int32"),
+    "off": ("sbuf", [128, 4, 16], "uint16"),
+    "xs": ("sbuf", [128, 2048], "bfloat16"),
+    "xg": ("sbuf", [128, 4096], "bfloat16"),
+    "ws": ("sbuf", [128, 2048], "bfloat16"),
+    "vs": ("sbuf", [128, 512], "bfloat16"),
+    "xq": ("sbuf", [128, 1024], Q8), "xp": ("sbuf", [128, 1024], "uint8"),
+    "wq": ("sbuf", [128, 512], Q8), "wp": ("sbuf", [128, 512], "uint8"),
+    "vq": ("sbuf", [128, 128], Q8), "vp": ("sbuf", [128, 128], "uint8"),
+    "rq": ("sbuf", [128, 256], Q8), "rp": ("sbuf", [128, 256], "uint8"),
+    "nq": ("sbuf", [128, 256], Q8), "np": ("sbuf", [128, 256], "uint8"),
+    "fq": ("sbuf", [128, 256], Q8), "fp": ("sbuf", [128, 256], "uint8"),
+    "h": ("sbuf", [128, 4, 512], "bfloat16"),
+    "hm": ("sbuf", [128, 4, 256], "bfloat16"),
+    "hq": ("sbuf", [128, 512], Q8), "hp": ("sbuf", [128, 512], "uint8"),
+    "yq": ("sbuf", [128, 1024], Q8), "yp": ("sbuf", [128, 1024], "uint8"),
+    "pls": ("sbuf", [128, 32], "int32"),
+    "pt": ("sbuf", [128, 10, 32], "int32"),
+    "yo": ("sbuf", [128, 32], "uint16"),
+    "ys": ("sbuf", [128, 1024], "float32"),
+    "yb": ("sbuf", [128, 512], "float32"),
+    "ps": ("psum", [128, 4096], "float32"),
+}
+SEMAPHORES = ["lt", "lx", "lw0", "lw", "lv", "lp", "lo", "ly", "cv", "cs", "ct", "snd",
+              "w0", "w1", "rx0", "rx1", "jn", "jf", "y0", "y1", "y2"]
+PLANE = {"xq": "xp", "wq": "wp", "rq": "rp", "nq": "np", "fq": "fp", "hq": "hp", "yq": "yp"}
+N = 8
+
+
+def make_plan(T, topo):
+    C = T.cores
+    par = [0 if topo.chip(C[r]) == topo.chip(C[0]) or topo.same_plane(C[r], C[0]) else 1 for r in range(N)]
+    die = [0 if topo.die(C[r]) == topo.die(C[0]) else 1 for r in range(N)]
+    hst = [0 if topo.host(C[r]) == topo.host(C[0]) else 1 for r in range(N)]
+    at = {(hst[r], par[r], die[r]): r for r in range(N)}
+    m1, m2 = [], []
+    for r in range(N):
+        far = [C[q] for q in range(N) if par[q] != par[r]][0]
+        port = [c for c in topo.cores_of(C[r]) if topo.die(c) == topo.die(C[r]) and c != C[r] and topo.may_write(c, far)]
+        m1.append(port[0])
+        m2.append(port[1])
+    S = {}
+    for a in range(N):
+        p, e, h = par[a], die[a], hst[a]
+        near = [b for b in range(N) if par[b] == p]
+        far = [b for b in range(N) if par[b] != p]
+        me = 64 * (2 * h + e)
+        S[C[a], "w0"] = [(m, "wq", 0, "wq", 0, 128, "w0") for m in (m1[a], m2[a])]
+        S[C[a], "w1"] = [(m, "wq", 128, "wq", 128, 384, "w1") for m in (m1[a], m2[a])]
+        S[C[a], "w2"] = [(m, "wp", 0, "wp", 0, 512, "w1") for m in (m1[a], m2[a])]
+        for d in (0, 1):
+            S[C[a], "xf%d" % d] = [(m, "xq", 256 * d + 128 * q, "rq", 128 * d, 128, "rx%d" % d) for q, m in ((0, m1[a]), (1, m2[a]))]
+            for q, m in ((0, m1[a]), (1, m2[a])):
+                to = [at[f, 1 - p, d] for f in (0, 1)]
+                S[m, "x%d" % d] = [(C[t] if q == par[t] else m2[t], "rq", 128 * d + 64 * f, "fq", me, 64, "jf") for f, t in enumerate(to)]
+        S[C[a], "xn"] = []
+        for f in (0, 1):
+            for d in (0, 1):
+                t = at[f, p, d]
+                for q in (0, 1):
+                    if (t, q) != (a, p):
+                        S[C[a], "xn"].append((C[t] if q == p else m1[t], "xq", 512 + 256 * d + 128 * q + 64 * f, "nq", me, 64, "jn"))
+        S[C[a], "h"] = [(C[b], "hq", 128 * j, "yq", 128 * (2 * h + e), 128, "y0") for j, b in enumerate(near) if b != a]
+        S[m1[a], "h"] = [(C[b], "hq", 64 * j, "yq", 512 + me, 64, "y1") for j, b in enumerate(far)]
+        S[m2[a], "h"] = [(C[b], "hq", 64 * j, "yq", 768 + me, 64, "y2") for j, b in enumerate(far)]
+    calls = {}
+    for (c, st), moves in S.items():
+        if st[0] == "w":
+            calls[c, st] = moves
+        else:
+            calls[c, st + "c"] = moves
+            calls[c, st + "s"] = [(d, PLANE[sb], sc, PLANE[db], dc, w, k) for d, sb, sc, db, dc, w, k in moves]
+    return dict(C=C, par=par, die=die, hst=hst, at=at, m1=m1, m2=m2, S=calls)
+
+
+def engines_of(core, moves, topo):
+    own = topo.cores_of(core)
+    off = [j for j, m in enumerate(moves) if m[0] not in own]
+    on = [j for j, m in enumerate(moves) if m[0] in own]
+    out = {}
+    e_off = topo.engines(core, moves[off[0]][0]) if off else []
+    for js, ok in ((off, e_off), (on, [k for k in topo.engines(core, moves[on[0]][0]) if k not in e_off] if on else [])):
+        per = 1
+        while js and 2 * per * len(js) <= len(ok):
+            per *= 2
+        for i, j in enumerate(js):
+            out[j] = ok[per * i:per * i + per]
+    return [out[j] for j in range(len(moves))]
+
+
+def rank_program(g, core, T, topo):
+    P = make_plan(T, topo)
+    S, C, par, die, hst, at = P["S"], P["C"], P["par"], P["die"], P["hst"], P["at"]
+    rank = T.rank_of(core)
+    helper = [k for k in ("m1", "m2") if core in P[k]]
+    if rank is None and not helper:
+        return
+    sem, V, A, X = T.sem, g.vector, g.scalar, g.tensor
+    ACT, OP = ActivationFunctionType, AluOpType
+    queue = {"cv": V, "cs": A}
+    H = T.h if rank is not None else T.hm
+
+    due = {}
+    for (c, st), moves in S.items():
+        for m, en in zip(moves, engines_of(c, moves, topo)):
+            if m[0] == core:
+                due[m[6]] = due.get(m[6], 0) + len(en)
+    n = {"cv": 0, "cs": 0, "ct": 0, "snd": 0}
+
+    def did(ins, s):
+        ins.then_inc(sem[s], 1)
+        n[s] += 1
+        return n[s]
+
+    def arrived(q, s):
+        q.wait_ge(sem[s], due[s])
+
+    def send(*calls):
+        for st in calls:
+            moves, tr = S[core, st], []
+            for (d, sb, sc, db, dc, w, s), e in zip(moves, engines_of(core, moves, topo)):
+                rid, pid = topo.addr(d, core)
+                src, dst = T[sb][:, sc:sc + w], T[db][:, dc:dc + w]
+                if sb in PLANE:
+                    src, dst = src.bitcast(dt.uint8), dst.bitcast(dt.uint8)
+                tr.append(RemoteDMATransfer(dst_ids=[DstId(rid=rid, pnc=pid)], dma_engine_mask=sum(1 << k for k in e),
+                                            remote_sem=sem[s], srcs=[src], dsts=[dst]))
+                n["snd"] += len(e)
+            g.remote_dma_fused(tr, local_sem=sem.snd)
+
+    def first_stage(src, w, bank0):
+        k = [did(X.matmul_mx(T.ps[:, 512 * (bank0 + i):512 * (bank0 + i) + 256], T.wq[:, 128 * i:128 * i + 128], T.wp[:, 128 * i:128 * i + 128],
+                             T[src][:, 0:256], T[PLANE[src]][:, 0:256], True, True), "ct") for i in range(4)]
+        for i in range(4):
+            s = ("cv", "cs")[i % 2]
+            queue[s].wait_ge(sem.ct, k[i])
+            for j in range(4):
+                c, in_ = 4 * (w + 16 * j), T.ps[:, 512 * (bank0 + i) + 64 * j:512 * (bank0 + i) + 64 * j + 64]
+                out = H[:, :, c + i:c + 64:4]
+                if s == "cv":
+                    did(V.tensor_scalar(out, in_, 0.0, 0.043, OP.max, OP.mult), "cv")
+                else:
+                    did(A.activation(out, in_, ACT.Relu, scale=0.043), "cs")
+
+    def pack_h(w):
+        V.wait_ge(sem.cv, n["cv"])
+        V.wait_ge(sem.cs, n["cs"])
+        return did(V.quantize_mx(T.hq[:, 0:4 * w], T.hp[:, 0:4 * w], H[:]), "cv")
+
+    def finish():
+        for s in ("cv", "cs", "ct", "snd"):
+            if n[s]:
+                g.wait_ge(sem[s], n[s])
+
+    if rank is None:
+        for d in (0, 1):
+            arrived(g, "rx%d" % d), send("x%dc" % d, "x%ds" % d)
+        arrived(X, "w0"), arrived(X, "w1")
+        x, s = ("nq", "jn") if helper[0] == "m1" else ("fq", "jf")
+        arrived(X, s)
+        first_stage(x, 0, 0)
+        g.wait_ge(sem.cv, pack_h(64))
+        send("hc", "hs")
+        return finish()
+
+    p, e, h = par[rank], die[rank], hst[rank]
+    g.scalar.dma_start(T.ws[:, 0:512], T.w[:, 0:512]).then_inc(sem.lw0, 16)
+    for k in range(8):
+        q = g.sync if k % 2 == 0 else g.scalar
+        q.dma_start(T.trs[16 * k:16 * k + 16, :, :, :, :], T.tri[:]).then_inc(sem.lt, 16)
+    g.sync.dma_start(T.xs[:], T.x[:]).then_inc(sem.lx, 16)
+    g.sync.dma_start(T.ws[:, 512:2048], T.w[:, 512:2048]).then_inc(sem.lw, 16)
+    g.sync.dma_start(T.vs[:], T.vv[:]).then_inc(sem.lv, 16)
+    for k in range(8):
+        g.sync.dma_start(T.pls[16 * k:16 * k + 16, :], T.plt[:]).then_inc(sem.lp, 16)
+    V.wait_ge(sem.lt, 128)
+    for k, (c, d) in enumerate(((1 - p, 0), (1 - p, 1), (p, 0), (p, 1))):
+        for q in (0, 1):
+            o_x = did(V.tensor_scalar(T.off[:, k, 8 * q:8 * q + 8], T.trs[:, :, c, 2 * d:2 * d + 2, 2 * q:2 * q + 2],
+                                      4.0, 0.0, OP.mult, OP.max), "cv")
+    V.wait_ge(sem.lw0, 16)
+    q_w0 = did(V.quantize_mx(T.wq[:, 0:128], T.wp[:, 0:128], T.ws[:, 0:512]), "cv")
+
+    def gather(s, j, t):
+        out, in_ = T.xg[:, 1024 * j + t:1024 * (j + 1):4], T.xs[:, t:2048].indirect(T.off[:, j, :])
+        if s == "cv":
+            return did(V.tensor_copy(out, in_), "cv")
+        return did(A.activation(out, in_, ACT.Copy), "cs")
+
+    for q in (V, A):
+        q.wait_ge(sem.lx, 16)
+        q.wait_ge(sem.cv, o_x)
+    ka = [[gather("cs", j, t) for t in ((2, 3) if j < 2 else (1, 2, 3))][-1] for j in range(4)]
+    q_x = []
+    for j in range(4):
+        kv = [gather("cv", j, t) for t in ((0, 1) if j < 2 else (0,))][-1]
+        V.wait_ge(sem.cs, ka[j])
+        V.wait_ge(sem.cv, kv)
+        q_x.append(did(V.quantize_mx(T.xq[:, 256 * j:256 * j + 256], T.xp[:, 256 * j:256 * j + 256], T.xg[:, 1024 * j:1024 * j + 1024]), "cv"))
+        if j == 1:
+            V.wait_ge(sem.lw, 16)
+            q_w = did(V.quantize_mx(T.wq[:, 128:512], T.wp[:, 128:512], T.ws[:, 512:2048]), "cv")
+    V.wait_ge(sem.lv, 16)
+    did(V.quantize_mx(T.vq[:], T.vp[:], T.vs[:]), "cv")
+
+    g.wait_ge(sem.cv, q_w0)
+    send("w0")
+    for d in (0, 1):
+        g.wait_ge(sem.cv, q_x[d])
+        send("xf%dc" % d, "xf%ds" % d)
+    g.wait_ge(sem.cv, q_x[3])
+    send("xnc", "xns")
+    send("w1", "w2")
+    g.sync.wait_ge(sem.cv, q_x[3])
+    c, me = 512 + 256 * e + 128 * p + 64 * h, 64 * (2 * h + e)
+    g.sync.dma_start(T.nq[:, me:me + 64].bitcast(dt.uint8), T.xq[:, c:c + 64].bitcast(dt.uint8)).then_inc(sem.lo, 16)
+    g.sync.dma_start(T.np[:, me:me + 64], T.xp[:, c:c + 64]).then_inc(sem.lo, 16)
+
+    V.wait_ge(sem.lp, 128)
+    pt = lambda k: T.pt[:, k, :]
+
+    def bits(k, b, m):
+        return did(V.tensor_scalar(pt(k), T.pls[:], b, m, OP.arith_shift_right, OP.bitwise_and), "cv")
+
+    def two(k, i, j, op):
+        return did(V.tensor_tensor(pt(k), pt(i), T.pls[:] if j is None else pt(j), op), "cv")
+
+    for k, b, m in ((0, 7, 7), (1, 4, 7), (2, 9, 1), (3, 8, 1)):
+        kk = bits(k, b, m)
+    V.wait_ge(sem.cv, kk)
+    two(4, 1, 0, OP.subtract)
+    kk = two(5, 3, 2, OP.subtract)
+    V.wait_ge(sem.cv, kk)
+    did(V.tensor_scalar(pt(6), pt(4), 112.0, None, OP.mult), "cv")
+    kk = did(V.tensor_scalar(pt(7), pt(5), 32.0, None, OP.mult), "cv")
+    V.wait_ge(sem.cv, kk)
+    kk = two(8, 6, 7, OP.add)
+    V.wait_ge(sem.cv, kk)
+    kk = two(9, 8, None, OP.add)
+    V.wait_ge(sem.cv, kk)
+    did(V.tensor_copy(T.yo[:], pt(9)), "cv")
+
+    X.wait_ge(sem.cv, q_w)
+    X.wait_ge(sem.lo, 32)
+    arrived(X, "jn")
+    first_stage("nq", 64 * p, 0)
+    arrived(X, "jf")
+    first_stage("fq", 64 * (1 - p), 4)
+    q_h = pack_h(128)
+    g.wait_ge(sem.cv, q_h)
+    send("hc", "hs")
+
+    near = [b for b in range(N) if par[b] == p]
+    far = [b for b in range(N) if par[b] != p]
+
+    def second_stage(bank, src, c, where):
+        k = did(X.matmul_mx(T.ps[:, 512 * bank:512 * bank + 128], T.vq[:], T.vp[:], T[src][:, c:c + 128], T[PLANE[src]][:, c:c + 128], True, True), "ct")
+        s = ("cv", "cs")[bank % 2]
+        queue[s].wait_ge(sem.ct, k)
+        for c0, w, to in where:
+            out, in_ = T.ys[:, to:to + w], T.ps[:, 512 * bank + c0:512 * bank + c0 + w]
+            if s == "cv":
+                did(V.tensor_copy(out, in_), "cv")
+            else:
+                did(A.activation(out, in_, ACT.Copy), "cs")
+
+    X.wait_ge(sem.cv, q_h)
+    X.wait_ge(sem.cs, n["cs"])
+    second_stage(0, "hq", 128 * near.index(rank), [(0, 128, 128 * rank)])
+    bank = 1
+    for s, base, ps in (("y1", 512, 1 - p), ("y0", 0, p), ("y2", 768, p)):
+        arrived(X, s)
+        if s == "y0":
+            for j, a in enumerate(near):
+                if a != rank:
+                    second_stage(bank, "yq", 128 * j, [(0, 128, 128 * a)])
+                    bank += 1
+        else:
+            for j in (0, 2):
+                second_stage(bank, "yq", base + 64 * j, [(64 * i, 64, 128 * far[j + i] + 64 * ps) for i in (0, 1)])
+                bank += 1
+    for q in (V, A):
+        q.wait_ge(sem.cv, n["cv"])
+        q.wait_ge(sem.cs, n["cs"])
+    kv = did(V.tensor_copy(T.yb[:, 0:256], T.ys[:].indirect(T.yo[:, 0:16])), "cv")
+    ks = did(A.activation(T.yb[:, 256:512], T.ys[:].indirect(T.yo[:, 16:32]), ACT.Copy), "cs")
+    g.sync.wait_ge(sem.cv, kv)
+    g.sync.dma_start(T.y[:, 0:256], T.yb[:, 0:256]).then_inc(sem.ly, 16)
+    A.wait_ge(sem.cs, ks)
+    A.dma_start(T.y[:, 256:512], T.yb[:, 256:512]).then_inc(sem.ly, 16)
+    g.wait_ge(sem.ly, 32)
+    finish()

@@ -3,33 +3,35 @@ from concourse.mybir import dt, AluOpType, ActivationFunctionType
 
 Q8 = "float8_e4m3fn_x4"
 SCRATCH = {
-    "trs": ("sbuf", [128, 2, 2, 4, 4], "int32"),
+    "trs": ("sbuf", [128, 16, 2, 2], "int32"),
     "off": ("sbuf", [128, 4, 16], "uint16"),
     "xs": ("sbuf", [128, 2048], "bfloat16"),
     "xg": ("sbuf", [128, 4096], "bfloat16"),
     "ws": ("sbuf", [128, 2048], "bfloat16"),
     "vs": ("sbuf", [128, 512], "bfloat16"),
-    "xq": ("sbuf", [128, 1024], Q8), "xp": ("sbuf", [128, 1024], "uint8"),
+    "xq": ("sbuf", [128, 896], Q8), "xp": ("sbuf", [128, 896], "uint8"),
     "wq": ("sbuf", [128, 512], Q8), "wp": ("sbuf", [128, 512], "uint8"),
     "vq": ("sbuf", [128, 128], Q8), "vp": ("sbuf", [128, 128], "uint8"),
-    "rq": ("sbuf", [128, 256], Q8), "rp": ("sbuf", [128, 256], "uint8"),
-    "nq": ("sbuf", [128, 256], Q8), "np": ("sbuf", [128, 256], "uint8"),
+    "rq": ("sbuf", [128, 128], Q8), "rp": ("sbuf", [128, 128], "uint8"),
+    "nq": ("sbuf", [128, 320], Q8), "np": ("sbuf", [128, 320], "uint8"),
     "fq": ("sbuf", [128, 256], Q8), "fp": ("sbuf", [128, 256], "uint8"),
-    "h": ("sbuf", [128, 4, 512], "bfloat16"),
-    "hm": ("sbuf", [128, 4, 256], "bfloat16"),
+    "h0": ("sbuf", [128, 4, 256], "bfloat16"),
+    "h1": ("sbuf", [128, 4, 256], "bfloat16"),
     "hq": ("sbuf", [128, 512], Q8), "hp": ("sbuf", [128, 512], "uint8"),
     "yq": ("sbuf", [128, 1024], Q8), "yp": ("sbuf", [128, 1024], "uint8"),
     "pls": ("sbuf", [128, 32], "int32"),
-    "pt": ("sbuf", [128, 10, 32], "int32"),
     "yo": ("sbuf", [128, 32], "uint16"),
+    "pt": ("sbuf", [128, 10, 32], "int32"),
     "ys": ("sbuf", [128, 1024], "float32"),
     "yb": ("sbuf", [128, 512], "float32"),
     "ps": ("psum", [128, 4096], "float32"),
 }
-SEMAPHORES = ["lt", "lx", "lw0", "lw", "lv", "lp", "lo", "ly", "cv", "cs", "ct", "snd",
-              "w0", "w1", "rx0", "rx1", "jn", "jf", "y0", "y1", "y2"]
+SEMAPHORES = ["lt", "lx", "lw0", "lw", "lv", "lp", "ly", "cv", "cs", "ct", "snd",
+              "w0", "w1", "w2", "rx", "jn", "jf", "y0", "y1", "y2", "y3"]
 PLANE = {"xq": "xp", "wq": "wp", "rq": "rp", "nq": "np", "fq": "fp", "hq": "hp", "yq": "yp"}
-N = 8
+N, WORLD = 8, 256
+SPLIT = (2, 3, 2, 3)
+POOL = {"w0": "all", "w1": "all", "x1": "hi", "x3": "hi", "we": "lo", "wf": "hi"}
 
 
 def make_plan(T, topo):
@@ -38,36 +40,48 @@ def make_plan(T, topo):
     die = [0 if topo.die(C[r]) == topo.die(C[0]) else 1 for r in range(N)]
     hst = [0 if topo.host(C[r]) == topo.host(C[0]) else 1 for r in range(N)]
     at = {(hst[r], par[r], die[r]): r for r in range(N)}
-    m1, m2 = [], []
+    assert all(at[h, p, d] == 4 * h + 2 * p + d for h, p, d in at)
+    m1, m2, mate = [], [], []
     for r in range(N):
         far = [C[q] for q in range(N) if par[q] != par[r]][0]
         port = [c for c in topo.cores_of(C[r]) if topo.die(c) == topo.die(C[r]) and c != C[r] and topo.may_write(c, far)]
         m1.append(port[0])
         m2.append(port[1])
-    S = {}
-    for a in range(N):
-        p, e, h = par[a], die[a], hst[a]
-        near = [b for b in range(N) if par[b] == p]
-        far = [b for b in range(N) if par[b] != p]
+        mate.append([c for c in range(WORLD) if topo.mates(c, C[r]) and topo.die(c) == topo.die(C[r]) and topo.may_write(c, C[r])])
+    S, relay = {}, {}
+
+    def slot(s, a):
+        j = 2 * (hst[s] ^ hst[a]) + (die[s] ^ die[a])
+        return 64 + 64 * j if die[a] else 192 - 64 * j
+
+    for s in range(N):
+        p, e, h = par[s], die[s], hst[s]
         me = 64 * (2 * h + e)
-        S[C[a], "w0"] = [(m, "wq", 0, "wq", 0, 128, "w0") for m in (m1[a], m2[a])]
-        S[C[a], "w1"] = [(m, "wq", 128, "wq", 128, 384, "w1") for m in (m1[a], m2[a])]
-        S[C[a], "w2"] = [(m, "wp", 0, "wp", 0, 512, "w1") for m in (m1[a], m2[a])]
-        for d in (0, 1):
-            S[C[a], "xf%d" % d] = [(m, "xq", 256 * d + 128 * q, "rq", 128 * d, 128, "rx%d" % d) for q, m in ((0, m1[a]), (1, m2[a]))]
-            for q, m in ((0, m1[a]), (1, m2[a])):
-                to = [at[f, 1 - p, d] for f in (0, 1)]
-                S[m, "x%d" % d] = [(C[t] if q == par[t] else m2[t], "rq", 128 * d + 64 * f, "fq", me, 64, "jf") for f, t in enumerate(to)]
-        S[C[a], "xn"] = []
-        for f in (0, 1):
+        S[C[s], "w0"] = [(m1[s], "wq", 0, "wq", 0, 64, "w0"), (m2[s], "wq", 64, "wq", 64, 64, "w0")]
+        S[m1[s], "we"] = [(m2[s], "wq", 0, "wq", 0, 64, "w1")]
+        S[m2[s], "we"] = [(m1[s], "wq", 64, "wq", 64, 64, "w1")]
+        for c, st, to in ((C[s], "w1", m1[s]), (m1[s], "wf", m2[s])):
+            S[c, st] = [(to, "wq", 128 * i, "wq", 128 * i, 128, "w2") for i in (1, 2, 3)] + [(to, "wp", 0, "wp", 0, 512, "w2")]
+        for j, f, via in ((0, 1 - h, mate[at[1 - h, 1 - p, e]]), (1, h, (m1[s], m2[s]))):
+            S[C[s], "x%d" % j] = [(via[d], "xq", 256 * j + 128 * d, "rq", 0, 128, "rx") for d in (0, 1)]
             for d in (0, 1):
-                t = at[f, p, d]
-                for q in (0, 1):
-                    if (t, q) != (a, p):
-                        S[C[a], "xn"].append((C[t] if q == p else m1[t], "xq", 512 + 256 * d + 128 * q + 64 * f, "nq", me, 64, "jn"))
-        S[C[a], "h"] = [(C[b], "hq", 128 * j, "yq", 128 * (2 * h + e), 128, "y0") for j, b in enumerate(near) if b != a]
-        S[m1[a], "h"] = [(C[b], "hq", 64 * j, "yq", 512 + me, 64, "y1") for j, b in enumerate(far)]
-        S[m2[a], "h"] = [(C[b], "hq", 64 * j, "yq", 768 + me, 64, "y2") for j, b in enumerate(far)]
+                a = at[f, 1 - p, d]
+                S.setdefault((via[0], "xr"), []).append((C[a], "rq", 64 * d, "fq", me, 64, "jf"))
+                S.setdefault((via[1], "xr"), []).append((m2[a], "rq", 64 * d, "fq", me, 64, "jf"))
+                relay[via[d]] = True
+        S[C[s], "x2"] = []
+        for d in (0, 1):
+            a = at[1 - h, p, d]
+            S[C[s], "x2"] += [(m1[a], "xq", 512 + 64 * d, "nq", slot(s, a), 64, "jn"), (C[a], "xq", 640 + 64 * d, "nq", slot(s, a), 64, "jn")]
+        a = at[h, p, 1 - e]
+        S[C[s], "x3"] = [(C[a], "nq", 256 * (1 - e), "nq", slot(s, a), 64, "jn"), (m1[a], "xq", 768 + 64 * (1 - e), "nq", slot(s, a), 64, "jn"),
+                         (m1[s], "xq", 768 + 64 * e, "nq", slot(s, s), 64, "jn")]
+        for k in (0, 1):
+            S[C[s], "h%d" % k] = [(C[at[1 - h, p, d]], "hq", 256 + 128 * k + 64 * d, "yq", 512 * k + (128 if d == e else 64 * h), 64, "y%d" % (2 * k))
+                                  for d in (0, 1)]
+            S[C[s], "h%d" % k].append((C[a], "hq", 128 * k + 64 * (1 - e), "yq", 512 * k + 64 * h, 64, "y%d" % (2 * k)))
+            S[(m1, m2)[k][s], "h"] = [(C[at[f, 1 - p, d]], "hq", 128 * f + 64 * d, "yq", 512 * k + 256 + 128 * e + 64 * h, 64, "y%d" % (2 * k + 1))
+                                      for f in (0, 1) for d in (0, 1)]
     calls = {}
     for (c, st), moves in S.items():
         if st[0] == "w":
@@ -75,21 +89,23 @@ def make_plan(T, topo):
         else:
             calls[c, st + "c"] = moves
             calls[c, st + "s"] = [(d, PLANE[sb], sc, PLANE[db], dc, w, k) for d, sb, sc, db, dc, w, k in moves]
-    return dict(C=C, par=par, die=die, hst=hst, at=at, m1=m1, m2=m2, S=calls)
+    return dict(C=C, par=par, die=die, hst=hst, at=at, m1=m1, m2=m2, relay=relay, S=calls)
 
 
-def engines_of(core, moves, topo):
+def engines_of(core, st, moves, topo, away):
     own = topo.cores_of(core)
-    off = [j for j, m in enumerate(moves) if m[0] not in own]
-    on = [j for j, m in enumerate(moves) if m[0] in own]
+    lo = topo.engines(core, away)
+    every = topo.engines(core, [c for c in own if c != core][0])
+    pool = {"lo": lo, "hi": [k for k in every if k not in lo], "all": every}[POOL.get(st[:2], "hi")]
     out = {}
-    e_off = topo.engines(core, moves[off[0]][0]) if off else []
-    for js, ok in ((off, e_off), (on, [k for k in topo.engines(core, moves[on[0]][0]) if k not in e_off] if on else [])):
-        per = 1
-        while js and 2 * per * len(js) <= len(ok):
-            per *= 2
+    for js, ok in (([j for j, m in enumerate(moves) if m[0] not in own], lo), ([j for j, m in enumerate(moves) if m[0] in own], pool)):
+        share = [1] * len(js)
+        k = 0
+        while js and sum(share) + share[k] <= len(ok):
+            share[k] *= 2
+            k = (k + 1) % len(js)
         for i, j in enumerate(js):
-            out[j] = ok[per * i:per * i + per]
+            out[j] = ok[sum(share[:i]):sum(share[:i + 1])]
     return [out[j] for j in range(len(moves))]
 
 
@@ -97,19 +113,21 @@ def rank_program(g, core, T, topo):
     P = make_plan(T, topo)
     S, C, par, die, hst, at = P["S"], P["C"], P["par"], P["die"], P["hst"], P["at"]
     rank = T.rank_of(core)
-    helper = [k for k in ("m1", "m2") if core in P[k]]
-    if rank is None and not helper:
+    if rank is None and core not in P["relay"]:
         return
     sem, V, A, X = T.sem, g.vector, g.scalar, g.tensor
     ACT, OP = ActivationFunctionType, AluOpType
     queue = {"cv": V, "cs": A}
-    H = T.h if rank is not None else T.hm
+
+    def engines(c, st):
+        return engines_of(c, st, S[c, st], topo, [r for r in C if topo.same_plane(c, r)][0])
 
     due = {}
     for (c, st), moves in S.items():
-        for m, en in zip(moves, engines_of(c, moves, topo)):
-            if m[0] == core:
-                due[m[6]] = due.get(m[6], 0) + len(en)
+        if any(m[0] == core for m in moves):
+            for m, en in zip(moves, engines(c, st)):
+                if m[0] == core:
+                    due[m[6]] = due.get(m[6], 0) + len(en)
     n = {"cv": 0, "cs": 0, "ct": 0, "snd": 0}
 
     def did(ins, s):
@@ -122,8 +140,8 @@ def rank_program(g, core, T, topo):
 
     def send(*calls):
         for st in calls:
-            moves, tr = S[core, st], []
-            for (d, sb, sc, db, dc, w, s), e in zip(moves, engines_of(core, moves, topo)):
+            tr = []
+            for (d, sb, sc, db, dc, w, s), e in zip(S[core, st], engines(core, st)):
                 rid, pid = topo.addr(d, core)
                 src, dst = T[sb][:, sc:sc + w], T[db][:, dc:dc + w]
                 if sb in PLANE:
@@ -133,24 +151,28 @@ def rank_program(g, core, T, topo):
                 n["snd"] += len(e)
             g.remote_dma_fused(tr, local_sem=sem.snd)
 
-    def first_stage(src, w, bank0):
+    def quantise(q, c, w, tile):
+        return did(V.quantize_mx(T[q][:, c:c + w], T[PLANE[q]][:, c:c + w], tile), "cv")
+
+    def first_stage(src, c0, order, H, bank0):
         k = [did(X.matmul_mx(T.ps[:, 512 * (bank0 + i):512 * (bank0 + i) + 256], T.wq[:, 128 * i:128 * i + 128], T.wp[:, 128 * i:128 * i + 128],
-                             T[src][:, 0:256], T[PLANE[src]][:, 0:256], True, True), "ct") for i in range(4)]
+                             T[src][:, c0:c0 + 256], T[PLANE[src]][:, c0:c0 + 256], True, True), "ct") for i in range(4)]
         for i in range(4):
             s = ("cv", "cs")[i % 2]
             queue[s].wait_ge(sem.ct, k[i])
             for j in range(4):
-                c, in_ = 4 * (w + 16 * j), T.ps[:, 512 * (bank0 + i) + 64 * j:512 * (bank0 + i) + 64 * j + 64]
+                c, in_ = 64 * order[j], T.ps[:, 512 * (bank0 + i) + 64 * j:512 * (bank0 + i) + 64 * j + 64]
                 out = H[:, :, c + i:c + 64:4]
                 if s == "cv":
                     did(V.tensor_scalar(out, in_, 0.0, 0.043, OP.max, OP.mult), "cv")
                 else:
                     did(A.activation(out, in_, ACT.Relu, scale=0.043), "cs")
-
-    def pack_h(w):
         V.wait_ge(sem.cv, n["cv"])
         V.wait_ge(sem.cs, n["cs"])
-        return did(V.quantize_mx(T.hq[:, 0:4 * w], T.hp[:, 0:4 * w], H[:]), "cv")
+
+    def near_order(a):
+        order = [2 * (hst[a] ^ (j >> 1)) + (die[a] ^ (j & 1)) for j in range(4)]
+        return order if die[a] else order[::-1]
 
     def finish():
         for s in ("cv", "cs", "ct", "snd"):
@@ -158,36 +180,42 @@ def rank_program(g, core, T, topo):
                 g.wait_ge(sem[s], n[s])
 
     if rank is None:
-        for d in (0, 1):
-            arrived(g, "rx%d" % d), send("x%dc" % d, "x%ds" % d)
-        arrived(X, "w0"), arrived(X, "w1")
-        x, s = ("nq", "jn") if helper[0] == "m1" else ("fq", "jf")
-        arrived(X, s)
-        first_stage(x, 0, 0)
-        g.wait_ge(sem.cv, pack_h(64))
-        send("hc", "hs")
+        first, second = core in P["m1"], core in P["m2"]
+        if first or second:
+            arrived(g, "w0"), send("we")
+        if first:
+            arrived(g, "w2"), send("wf")
+        arrived(g, "rx"), send("xrc", "xrs")
+        if first or second:
+            arrived(X, "w0"), arrived(X, "w1"), arrived(X, "w2")
+            if first:
+                a = P["m1"].index(core)
+                arrived(X, "jn"), first_stage("nq", 64 * die[a], near_order(a), T.h0, 0)
+            else:
+                arrived(X, "jf"), first_stage("fq", 0, range(4), T.h0, 0)
+            g.wait_ge(sem.cv, quantise("hq", 0, 256, T.h0[:]))
+            send("hc", "hs")
         return finish()
 
     p, e, h = par[rank], die[rank], hst[rank]
+    g.sync.dma_start(T.trs[0:16, :, :, :], T.tri[:]).then_inc(sem.lt, 16)
+    g.scalar.dma_start(T.trs[16:32, :, :, :], T.tri[:]).then_inc(sem.lt, 16)
     g.scalar.dma_start(T.ws[:, 0:512], T.w[:, 0:512]).then_inc(sem.lw0, 16)
-    for k in range(8):
-        q = g.sync if k % 2 == 0 else g.scalar
-        q.dma_start(T.trs[16 * k:16 * k + 16, :, :, :, :], T.tri[:]).then_inc(sem.lt, 16)
     g.sync.dma_start(T.xs[:], T.x[:]).then_inc(sem.lx, 16)
     g.sync.dma_start(T.ws[:, 512:2048], T.w[:, 512:2048]).then_inc(sem.lw, 16)
-    g.sync.dma_start(T.vs[:], T.vv[:]).then_inc(sem.lv, 16)
     for k in range(8):
         g.sync.dma_start(T.pls[16 * k:16 * k + 16, :], T.plt[:]).then_inc(sem.lp, 16)
-    V.wait_ge(sem.lt, 128)
-    for k, (c, d) in enumerate(((1 - p, 0), (1 - p, 1), (p, 0), (p, 1))):
-        for q in (0, 1):
-            o_x = did(V.tensor_scalar(T.off[:, k, 8 * q:8 * q + 8], T.trs[:, :, c, 2 * d:2 * d + 2, 2 * q:2 * q + 2],
-                                      4.0, 0.0, OP.mult, OP.max), "cv")
+    V.wait_ge(sem.lt, 32)
+    for q in range(4):
+        for k, c in enumerate((1 - p, p)):
+            o_x = did(V.tensor_scalar(T.off[32 * q:32 * q + 32, :, 8 * k:8 * k + 8], T.trs[0:32, :, c, :], 4.0, 0.0, OP.mult, OP.max), "cv")
     V.wait_ge(sem.lw0, 16)
-    q_w0 = did(V.quantize_mx(T.wq[:, 0:128], T.wp[:, 0:128], T.ws[:, 0:512]), "cv")
+    q_w0 = quantise("wq", 0, 128, T.ws[:, 0:512])
+
+    chips = [at[1 - h, 1 - p, 0], at[h, 1 - p, 0], at[1 - h, p, 0], at[h, p, 0]]
 
     def gather(s, j, t):
-        out, in_ = T.xg[:, 1024 * j + t:1024 * (j + 1):4], T.xs[:, t:2048].indirect(T.off[:, j, :])
+        out, in_ = T.xg[:, 1024 * j + t:1024 * (j + 1):4], T.xs[:, t:2048].indirect(T.off[:, chips[j] // 2, :])
         if s == "cv":
             return did(V.tensor_copy(out, in_), "cv")
         return did(A.activation(out, in_, ACT.Copy), "cs")
@@ -195,95 +223,85 @@ def rank_program(g, core, T, topo):
     for q in (V, A):
         q.wait_ge(sem.lx, 16)
         q.wait_ge(sem.cv, o_x)
-    ka = [[gather("cs", j, t) for t in ((2, 3) if j < 2 else (1, 2, 3))][-1] for j in range(4)]
+    ka = [[gather("cs", j, t) for t in range(4 - SPLIT[j], 4)][-1] for j in range(4)]
     q_x = []
     for j in range(4):
-        kv = [gather("cv", j, t) for t in ((0, 1) if j < 2 else (0,))][-1]
+        kv = [gather("cv", j, t) for t in range(4 - SPLIT[j])][-1]
         V.wait_ge(sem.cs, ka[j])
         V.wait_ge(sem.cv, kv)
-        q_x.append(did(V.quantize_mx(T.xq[:, 256 * j:256 * j + 256], T.xp[:, 256 * j:256 * j + 256], T.xg[:, 1024 * j:1024 * j + 1024]), "cv"))
-        if j == 1:
+        if j < 3:
+            q_x.append(quantise("xq", 256 * j, 256, T.xg[:, 1024 * j:1024 * j + 1024]))
+        else:
+            quantise("xq", 768, 128, T.xg[:, 3072:3584])
+            q_x.append(quantise("nq", 192 * (1 - e), 128, T.xg[:, 3584:4096]))
+        if j == 0:
             V.wait_ge(sem.lw, 16)
-            q_w = did(V.quantize_mx(T.wq[:, 128:512], T.wp[:, 128:512], T.ws[:, 512:2048]), "cv")
-    V.wait_ge(sem.lv, 16)
-    did(V.quantize_mx(T.vq[:], T.vp[:], T.vs[:]), "cv")
-
-    g.wait_ge(sem.cv, q_w0)
-    send("w0")
-    for d in (0, 1):
-        g.wait_ge(sem.cv, q_x[d])
-        send("xf%dc" % d, "xf%ds" % d)
-    g.wait_ge(sem.cv, q_x[3])
-    send("xnc", "xns")
-    send("w1", "w2")
-    g.sync.wait_ge(sem.cv, q_x[3])
-    c, me = 512 + 256 * e + 128 * p + 64 * h, 64 * (2 * h + e)
-    g.sync.dma_start(T.nq[:, me:me + 64].bitcast(dt.uint8), T.xq[:, c:c + 64].bitcast(dt.uint8)).then_inc(sem.lo, 16)
-    g.sync.dma_start(T.np[:, me:me + 64], T.xp[:, c:c + 64]).then_inc(sem.lo, 16)
+            q_w = quantise("wq", 128, 384, T.ws[:, 512:2048])
+    g.sync.wait_ge(sem.cv, q_x[2])
+    g.sync.dma_start(T.vs[:], T.vv[:]).then_inc(sem.lv, 16)
 
     V.wait_ge(sem.lp, 128)
     pt = lambda k: T.pt[:, k, :]
-
-    def bits(k, b, m):
-        return did(V.tensor_scalar(pt(k), T.pls[:], b, m, OP.arith_shift_right, OP.bitwise_and), "cv")
-
-    def two(k, i, j, op):
-        return did(V.tensor_tensor(pt(k), pt(i), T.pls[:] if j is None else pt(j), op), "cv")
-
-    for k, b, m in ((0, 7, 7), (1, 4, 7), (2, 9, 1), (3, 8, 1)):
-        kk = bits(k, b, m)
-    V.wait_ge(sem.cv, kk)
-    two(4, 1, 0, OP.subtract)
-    kk = two(5, 3, 2, OP.subtract)
-    V.wait_ge(sem.cv, kk)
-    did(V.tensor_scalar(pt(6), pt(4), 112.0, None, OP.mult), "cv")
-    kk = did(V.tensor_scalar(pt(7), pt(5), 32.0, None, OP.mult), "cv")
-    V.wait_ge(sem.cv, kk)
-    kk = two(8, 6, 7, OP.add)
-    V.wait_ge(sem.cv, kk)
-    kk = two(9, 8, None, OP.add)
+    up = did(V.tensor_scalar(pt(0), T.pls[:], 8.0, None, OP.mult), "cv")
+    for k, b, m in ((1, 0, 64 + 15), (2, 4, 32), (3, 3, 16)):
+        did(V.tensor_scalar(pt(k), T.pls[:], b, m, OP.arith_shift_right, OP.bitwise_and), "cv")
+    V.wait_ge(sem.cv, up)
+    for k, b, m in ((4, 0, 256 + 128), (5, 2, 512)):
+        kk = did(V.tensor_scalar(pt(k), pt(0), b, m, OP.arith_shift_right, OP.bitwise_and), "cv")
+    for step in (((6, 1, 2), (7, 3, 4)), ((8, 5, 6),), ((9, 7, 8),)):
+        V.wait_ge(sem.cv, kk)
+        for k, i, j in step:
+            kk = did(V.tensor_tensor(pt(k), pt(i), pt(j), OP.add), "cv")
     V.wait_ge(sem.cv, kk)
     did(V.tensor_copy(T.yo[:], pt(9)), "cv")
 
-    X.wait_ge(sem.cv, q_w)
-    X.wait_ge(sem.lo, 32)
-    arrived(X, "jn")
-    first_stage("nq", 64 * p, 0)
-    arrived(X, "jf")
-    first_stage("fq", 64 * (1 - p), 4)
-    q_h = pack_h(128)
-    g.wait_ge(sem.cv, q_h)
-    send("hc", "hs")
+    g.wait_ge(sem.cv, q_w0)
+    send("w0")
+    g.wait_ge(sem.cv, q_x[0])
+    send("x0c", "x0s")
+    g.wait_ge(sem.cv, q_w)
+    send("w1")
+    for j in (1, 2, 3):
+        g.wait_ge(sem.cv, q_x[j])
+        send("x%dc" % j, "x%ds" % j)
 
-    near = [b for b in range(N) if par[b] == p]
-    far = [b for b in range(N) if par[b] != p]
+    X.wait_ge(sem.cv, q_x[3])
+    for k, (s, src, c0, order, H) in enumerate((("jn", "nq", 64 * e, near_order(rank), T.h0), ("jf", "fq", 0, range(4), T.h1))):
+        arrived(X, s)
+        first_stage(src, c0, order, H, 4 * k)
+        quantise("hq", 256 + 128 * k, 128, H[:, 2 - 2 * h:4 - 2 * h, :])
+        q_h = quantise("hq", 128 * k, 128, H[:, 2 * h:2 * h + 2, :])
+        g.wait_ge(sem.cv, q_h)
+        send("h%dc" % k, "h%ds" % k)
+    V.wait_ge(sem.lv, 16)
+    q_v = did(V.quantize_mx(T.vq[:], T.vp[:], T.vs[:]), "cv")
 
-    def second_stage(bank, src, c, where):
-        k = did(X.matmul_mx(T.ps[:, 512 * bank:512 * bank + 128], T.vq[:], T.vp[:], T[src][:, c:c + 128], T[PLANE[src]][:, c:c + 128], True, True), "ct")
-        s = ("cv", "cs")[bank % 2]
+    def second_stage(bank, src, c, w, s, where):
+        k = did(X.matmul_mx(T.ps[:, 512 * bank:512 * bank + w], T.vq[:], T.vp[:], T[src][:, c:c + w], T[PLANE[src]][:, c:c + w], True, True), "ct")
         queue[s].wait_ge(sem.ct, k)
-        for c0, w, to in where:
+        for c0, w, a, ps in where:
+            to = 512 * ps + 256 * par[a] + 128 * die[a] + 64 * hst[a]
             out, in_ = T.ys[:, to:to + w], T.ps[:, 512 * bank + c0:512 * bank + c0 + w]
             if s == "cv":
-                did(V.tensor_copy(out, in_), "cv")
+                k = did(V.tensor_copy(out, in_), "cv")
             else:
-                did(A.activation(out, in_, ACT.Copy), "cs")
+                k = did(A.activation(out, in_, ACT.Copy), "cs")
+        return k
 
-    X.wait_ge(sem.cv, q_h)
+    X.wait_ge(sem.cv, q_v)
     X.wait_ge(sem.cs, n["cs"])
-    second_stage(0, "hq", 128 * near.index(rank), [(0, 128, 128 * rank)])
-    bank = 1
-    for s, base, ps in (("y1", 512, 1 - p), ("y0", 0, p), ("y2", 768, p)):
-        arrived(X, s)
-        if s == "y0":
-            for j, a in enumerate(near):
-                if a != rank:
-                    second_stage(bank, "yq", 128 * j, [(0, 128, 128 * a)])
-                    bank += 1
+    own = second_stage(0, "hq", 0, 256, "cs", [(64 * e, 64, rank, p), (128 + 64 * e, 64, rank, 1 - p)])
+    for k in range(4):
+        arrived(X, "y%d" % k)
+        ps = p if k in (0, 3) else 1 - p
+        if k % 2 == 0:
+            second_stage(2 * k + 1, "yq", 256 * k, 128, "cv", [(0, 128, at[0, p, 1 - e], ps)])
+            second_stage(2 * k + 2, "yq", 256 * k + 64, 128, "cs", [(64, 64, at[1 - h, p, e], ps)])
         else:
-            for j in (0, 2):
-                second_stage(bank, "yq", base + 64 * j, [(64 * i, 64, 128 * far[j + i] + 64 * ps) for i in (0, 1)])
-                bank += 1
+            second_stage(2 * k + 1, "yq", 256 * k, 128, "cv", [(0, 128, at[0, 1 - p, 0], ps)])
+            if k == 3:
+                X.wait_ge(sem.cs, own)
+            second_stage((2 * k + 2) % 8, "yq", 256 * k + 128, 128, "cs", [(0, 128, at[0, 1 - p, 1], ps)])
     for q in (V, A):
         q.wait_ge(sem.cv, n["cv"])
         q.wait_ge(sem.cs, n["cs"])

@@ -3,16 +3,16 @@ from concourse.mybir import dt, AluOpType, ActivationFunctionType
 
 Q8 = "float8_e4m3fn_x4"
 SCRATCH = {
-    "trs": ("sbuf", [128, 16, 2, 2], "int32"),
+    "trs": ("sbuf", [128, 2, 2, 4, 2, 2], "int32"),
     "off": ("sbuf", [128, 4, 16], "uint16"),
     "xs": ("sbuf", [128, 2048], "bfloat16"),
     "xg": ("sbuf", [128, 4096], "bfloat16"),
     "ws": ("sbuf", [128, 2048], "bfloat16"),
     "vs": ("sbuf", [128, 512], "bfloat16"),
-    "xq": ("sbuf", [128, 896], Q8), "xp": ("sbuf", [128, 896], "uint8"),
+    "xq": ("sbuf", [128, 1024], Q8), "xp": ("sbuf", [128, 1024], "uint8"),
     "wq": ("sbuf", [128, 512], Q8), "wp": ("sbuf", [128, 512], "uint8"),
     "vq": ("sbuf", [128, 128], Q8), "vp": ("sbuf", [128, 128], "uint8"),
-    "rq": ("sbuf", [128, 128], Q8), "rp": ("sbuf", [128, 128], "uint8"),
+    "rq": ("sbuf", [128, 256], Q8), "rp": ("sbuf", [128, 256], "uint8"),
     "nq": ("sbuf", [128, 320], Q8), "np": ("sbuf", [128, 320], "uint8"),
     "fq": ("sbuf", [128, 256], Q8), "fp": ("sbuf", [128, 256], "uint8"),
     "h0": ("sbuf", [128, 4, 256], "bfloat16"),
@@ -27,11 +27,12 @@ SCRATCH = {
     "ps": ("psum", [128, 4096], "float32"),
 }
 SEMAPHORES = ["lt", "lx", "lw0", "lw", "lv", "lp", "ly", "cv", "cs", "ct", "snd",
-              "w0", "w1", "w2", "rx", "jn", "jf", "y0", "y1", "y2", "y3"]
-PLANE = {"xq": "xp", "wq": "wp", "rq": "rp", "nq": "np", "fq": "fp", "hq": "hp", "yq": "yp"}
+              "w0", "w1", "w2", "w3", "rC", "rD", "jn", "jf", "yA", "yB", "yC", "yD", "yT"]
+PLANE = {"xq": "xp", "wq": "wp", "vq": "vp", "rq": "rp", "nq": "np", "fq": "fp", "hq": "hp", "yq": "yp"}
 N, WORLD = 8, 256
-SPLIT = (2, 3, 2, 3)
-POOL = {"w0": "all", "w1": "all", "x1": "hi", "x3": "hi", "we": "lo", "wf": "hi"}
+JOBS = {"A": (True, True), "B": (True, False), "C": (False, True), "D": (False, False)}
+OPT = dict(gather="DCBA", rank="AC", last="BATDC", two=1, tri=(0, 1, 0, 0), shape=((0, 0, 256), (1, 0, 256), (2, 0, 128), (2, 128, 128), (3, 0, 128), (3, 128, 128)), split=(2, 3, 2, 3, 4), w="m1", wafter=0, stores=4, via="host", tsplit="", dm=False, early=1, w0="swap",
+           pool={"w0": "all", "w1": "all", "we": "lo", "wf": "all"})
 
 
 def make_plan(T, topo):
@@ -48,7 +49,10 @@ def make_plan(T, topo):
         m1.append(port[0])
         m2.append(port[1])
         mate.append([c for c in range(WORLD) if topo.mates(c, C[r]) and topo.die(c) == topo.die(C[r]) and topo.may_write(c, C[r])])
+    dm = [m[0] for m in mate] if OPT["dm"] else m2
     S, relay = {}, {}
+    x0 = {job: 256 * j for j, job in enumerate(OPT["gather"])}
+    y0 = {job: 256 * j for j, job in enumerate("ABCD")}
 
     def slot(s, a):
         j = 2 * (hst[s] ^ hst[a]) + (die[s] ^ die[a])
@@ -56,32 +60,53 @@ def make_plan(T, topo):
 
     for s in range(N):
         p, e, h = par[s], die[s], hst[s]
-        me = 64 * (2 * h + e)
-        S[C[s], "w0"] = [(m1[s], "wq", 0, "wq", 0, 64, "w0"), (m2[s], "wq", 64, "wq", 64, 64, "w0")]
-        S[m1[s], "we"] = [(m2[s], "wq", 0, "wq", 0, 64, "w1")]
-        S[m2[s], "we"] = [(m1[s], "wq", 64, "wq", 64, 64, "w1")]
-        for c, st, to in ((C[s], "w1", m1[s]), (m1[s], "wf", m2[s])):
-            S[c, st] = [(to, "wq", 128 * i, "wq", 128 * i, 128, "w2") for i in (1, 2, 3)] + [(to, "wp", 0, "wp", 0, 512, "w2")]
-        for j, f, via in ((0, 1 - h, mate[at[1 - h, 1 - p, e]]), (1, h, (m1[s], m2[s]))):
-            S[C[s], "x%d" % j] = [(via[d], "xq", 256 * j + 128 * d, "rq", 0, 128, "rx") for d in (0, 1)]
-            for d in (0, 1):
-                a = at[f, 1 - p, d]
-                S.setdefault((via[0], "xr"), []).append((C[a], "rq", 64 * d, "fq", me, 64, "jf"))
-                S.setdefault((via[1], "xr"), []).append((m2[a], "rq", 64 * d, "fq", me, 64, "jf"))
-                relay[via[d]] = True
-        S[C[s], "x2"] = []
-        for d in (0, 1):
-            a = at[1 - h, p, d]
-            S[C[s], "x2"] += [(m1[a], "xq", 512 + 64 * d, "nq", slot(s, a), 64, "jn"), (C[a], "xq", 640 + 64 * d, "nq", slot(s, a), 64, "jn")]
-        a = at[h, p, 1 - e]
-        S[C[s], "x3"] = [(C[a], "nq", 256 * (1 - e), "nq", slot(s, a), 64, "jn"), (m1[a], "xq", 768 + 64 * (1 - e), "nq", slot(s, a), 64, "jn"),
-                         (m1[s], "xq", 768 + 64 * e, "nq", slot(s, s), 64, "jn")]
-        for k in (0, 1):
-            S[C[s], "h%d" % k] = [(C[at[1 - h, p, d]], "hq", 256 + 128 * k + 64 * d, "yq", 512 * k + (128 if d == e else 64 * h), 64, "y%d" % (2 * k))
-                                  for d in (0, 1)]
-            S[C[s], "h%d" % k].append((C[a], "hq", 128 * k + 64 * (1 - e), "yq", 512 * k + 64 * h, 64, "y%d" % (2 * k)))
-            S[(m1, m2)[k][s], "h"] = [(C[at[f, 1 - p, d]], "hq", 128 * f + 64 * d, "yq", 512 * k + 256 + 128 * e + 64 * h, 64, "y%d" % (2 * k + 1))
-                                      for f in (0, 1) for d in (0, 1)]
+        me, twin = 64 * (2 * h + e), at[h, p, 1 - e]
+        we = OPT["early"]
+        tiles = [("wq", 128 * i, "wq", 128 * i, 128) for i in range(4)] + [("wp", 0, "wp", 0, 512)]
+        early, rest = (tiles[:we], tiles[we:]) if we < 4 else (tiles, [])
+        if we == 1:
+            early = [("wq", 64 * i, "wq", 64 * i, 64) for i in (0, 1)]
+        for parts, go, on, s0, s1, mode in ((early, "w0", "we", "w0", "w1", OPT["w0"]), (rest, "w1", "wf", "w2", "w3", OPT["w"])):
+            if not parts:
+                continue
+            k = {"swap": len(parts) // 2, "m1": len(parts), "m2": 0, "both": 0}[mode]
+            if mode == "both":
+                S[C[s], go] = [(m,) + r + (s0,) for m in (m1[s], m2[s]) for r in parts]
+                if OPT["dm"]:
+                    S[m2[s], on] = [(dm[s],) + r + (s1,) for r in parts]
+                continue
+            S[C[s], go] = [((m1[s], m2[s])[i >= k],) + r + (s0,) for i, r in enumerate(parts)]
+            if parts[:k]:
+                S[m1[s], on] = [(dm[s],) + r + (s1,) for r in parts[:k]]
+            if parts[k:]:
+                S[m2[s], on] = [(c,) + r + (s1,) for c in (dm[s], m1[s]) if c != m2[s] for r in parts[k:]]
+        if OPT["dm"]:
+            S[C[s], "xD"] = [(dm[at[f, 1 - p, d]], "xq", x0["D"] + 128 * f + 64 * d, "fq", me, 64, "jf") for f in (0, 1) for d in (0, 1)]
+            relay[m1[s]] = None
+        for k, job, to in ((0, "C", C), (1, "D", m2))[:2 - OPT["dm"]]:
+            k = (k, 0)[OPT["dm"]]
+            S[C[s], "x" + job] = []
+            ways = ((1 - h, mate[at[1 - h, 1 - p, e]][k * OPT["two"]]), (h, (m1, m2)[k or OPT["dm"]][s]))
+            if OPT["via"] == "job":
+                ways = [(f, mate[at[f, 1 - p, e]][h] if job == OPT["gather"][0] else (m1, m2)[f][s]) for f in (1 - h, h)]
+            if OPT["via"] == "src" or (OPT["via"] == "half" and job != OPT["gather"][0]):
+                ways = ((1 - h, (m2, m1)[k][s]), (h, (m1, m2)[k][s]))
+            if OPT["via"] == "mate":
+                ways = [(f, mate[at[f, 1 - p, e]][h]) for f in (1 - h, h)]
+                relay[m1[s]] = relay[m2[s]] = None
+            for f, via in ways:
+                S[C[s], "x" + job].append((via, "xq", x0[job] + 128 * f, "rq", 128 * k, 128, "r" + job))
+                S[via, "r" + job] = [(to[at[f, 1 - p, d]], "rq", 128 * k + 64 * d, "fq", me, 64, "jf") for d in (0, 1)]
+                relay[via] = job
+        near = [at[f, p, d] for f in (0, 1) for d in (0, 1)]
+        S[C[s], "xB"] = [(m1[a], "xq", x0["B"] + 64 * j, "nq", slot(s, a), 64, "jn") for j, a in enumerate(near)]
+        S[C[s], "xA"] = [(C[a], "xq", x0["A"] + 64 * j, "nq", slot(s, a), 64, "jn") for j, a in ((2 - 2 * e, at[1 - h, p, 0]), (3 - 2 * e, at[1 - h, p, 1]), (1 + e, twin))]
+        for k, job in enumerate("AC"):
+            S[C[s], "h" + job] = [(C[at[1 - h, p, d]], "hq", 256 + 128 * k + 64 * d, "yq", y0[job] + 64 * e, 64, "y" + job) for d in (0, 1)]
+            S.setdefault((C[s], ("t" if job in OPT["tsplit"] else "h") + job), []).append(
+                (C[twin], "hq", 128 * k + 64 * (1 - e), "yq", y0["A"] + 128 + 64 * k, 64, "yT"))
+        for m, job in ((m1, "B"), (dm, "D")):
+            S[m[s], "h"] = [(C[at[f, 1 - p, d]], "hq", 128 * f + 64 * d, "yq", y0[job] + 128 * e + 64 * h, 64, "y" + job) for f in (0, 1) for d in (0, 1)]
     calls = {}
     for (c, st), moves in S.items():
         if st[0] == "w":
@@ -89,14 +114,14 @@ def make_plan(T, topo):
         else:
             calls[c, st + "c"] = moves
             calls[c, st + "s"] = [(d, PLANE[sb], sc, PLANE[db], dc, w, k) for d, sb, sc, db, dc, w, k in moves]
-    return dict(C=C, par=par, die=die, hst=hst, at=at, m1=m1, m2=m2, relay=relay, S=calls)
+    return dict(C=C, par=par, die=die, hst=hst, at=at, m1=m1, dm=dm, relay=relay, S=calls, x0=x0, y0=y0)
 
 
 def engines_of(core, st, moves, topo, away):
     own = topo.cores_of(core)
     lo = topo.engines(core, away)
     every = topo.engines(core, [c for c in own if c != core][0])
-    pool = {"lo": lo, "hi": [k for k in every if k not in lo], "all": every}[POOL.get(st[:2], "hi")]
+    pool = {"lo": lo, "hi": [k for k in every if k not in lo], "all": every}[OPT["pool"].get(st[:2], "hi")]
     out = {}
     for js, ok in (([j for j, m in enumerate(moves) if m[0] not in own], lo), ([j for j, m in enumerate(moves) if m[0] in own], pool)):
         share = [1] * len(js)
@@ -136,7 +161,8 @@ def rank_program(g, core, T, topo):
         return n[s]
 
     def arrived(q, s):
-        q.wait_ge(sem[s], due[s])
+        if s in due:
+            q.wait_ge(sem[s], due[s])
 
     def send(*calls):
         for st in calls:
@@ -154,19 +180,29 @@ def rank_program(g, core, T, topo):
     def quantise(q, c, w, tile):
         return did(V.quantize_mx(T[q][:, c:c + w], T[PLANE[q]][:, c:c + w], tile), "cv")
 
-    def first_stage(src, c0, order, H, bank0):
-        k = [did(X.matmul_mx(T.ps[:, 512 * (bank0 + i):512 * (bank0 + i) + 256], T.wq[:, 128 * i:128 * i + 128], T.wp[:, 128 * i:128 * i + 128],
-                             T[src][:, c0:c0 + 256], T[PLANE[src]][:, c0:c0 + 256], True, True), "ct") for i in range(4)]
-        for i in range(4):
-            s = ("cv", "cs")[i % 2]
-            queue[s].wait_ge(sem.ct, k[i])
-            for j in range(4):
-                c, in_ = 64 * order[j], T.ps[:, 512 * (bank0 + i) + 64 * j:512 * (bank0 + i) + 64 * j + 64]
+    read = []
+
+    def product(w, q, i, src, c):
+        k = len(read)
+        if k >= 8:
+            X.wait_ge(sem[read[k - 8][0]], read[k - 8][1])
+        kk = did(X.matmul_mx(T.ps[:, 512 * (k % 8):512 * (k % 8) + w], T[q][:, 128 * i:128 * i + 128], T[PLANE[q]][:, 128 * i:128 * i + 128],
+                             T[src][:, c:c + w], T[PLANE[src]][:, c:c + w], True, True), "ct")
+        s = ("cv", "cs")[k % 2]
+        queue[s].wait_ge(sem.ct, kk)
+        return k % 8, s
+
+    def first_stage(src, c0, order, H):
+        for i, u, w in OPT["shape"]:
+            bank, s = product(w, "wq", i, src, c0 + u)
+            for j in range(w // 64):
+                c, in_ = 64 * order[u // 64 + j], T.ps[:, 512 * bank + 64 * j:512 * bank + 64 * j + 64]
                 out = H[:, :, c + i:c + 64:4]
                 if s == "cv":
                     did(V.tensor_scalar(out, in_, 0.0, 0.043, OP.max, OP.mult), "cv")
                 else:
                     did(A.activation(out, in_, ACT.Relu, scale=0.043), "cs")
+            read.append((s, n[s]))
         V.wait_ge(sem.cv, n["cv"])
         V.wait_ge(sem.cs, n["cs"])
 
@@ -180,42 +216,56 @@ def rank_program(g, core, T, topo):
                 g.wait_ge(sem[s], n[s])
 
     if rank is None:
-        first, second = core in P["m1"], core in P["m2"]
-        if first or second:
+        first, second = core in P["m1"], core in P["dm"]
+        if (core, "we") in S:
             arrived(g, "w0"), send("we")
-        if first:
-            arrived(g, "w2"), send("wf")
-        arrived(g, "rx"), send("xrc", "xrs")
+        steps = [("r" + job, ("r%sc" % job, "r%ss" % job)) for job in OPT["gather"]]
+        steps.insert(OPT["wafter"] + 1, ("w2", ("wf",)))
+        for s, calls in steps:
+            if (core, calls[0]) in S:
+                arrived(g, s), send(*calls)
         if first or second:
-            arrived(X, "w0"), arrived(X, "w1"), arrived(X, "w2")
+            for s in ("w0", "w1", "w2", "w3"):
+                arrived(X, s)
             if first:
                 a = P["m1"].index(core)
-                arrived(X, "jn"), first_stage("nq", 64 * die[a], near_order(a), T.h0, 0)
+                arrived(X, "jn"), first_stage("nq", 64 * die[a], near_order(a), T.h0)
             else:
-                arrived(X, "jf"), first_stage("fq", 0, range(4), T.h0, 0)
+                arrived(X, "jf"), first_stage("fq", 0, range(4), T.h0)
             g.wait_ge(sem.cv, quantise("hq", 0, 256, T.h0[:]))
             send("hc", "hs")
         return finish()
 
     p, e, h = par[rank], die[rank], hst[rank]
-    g.sync.dma_start(T.trs[0:16, :, :, :], T.tri[:]).then_inc(sem.lt, 16)
-    g.scalar.dma_start(T.trs[16:32, :, :, :], T.tri[:]).then_inc(sem.lt, 16)
-    g.scalar.dma_start(T.ws[:, 0:512], T.w[:, 0:512]).then_inc(sem.lw0, 16)
+    we, R = OPT["early"], 16 * len(OPT["tri"])
+    g.scalar.dma_start(T.ws[:, 0:512 * we], T.w[:, 0:512 * we]).then_inc(sem.lw0, 16)
+    for k, q in enumerate(OPT["tri"]):
+        (g.sync, g.scalar)[q].dma_start(T.trs[16 * k:16 * k + 16], T.tri[:]).then_inc(sem.lt, 16)
     g.sync.dma_start(T.xs[:], T.x[:]).then_inc(sem.lx, 16)
-    g.sync.dma_start(T.ws[:, 512:2048], T.w[:, 512:2048]).then_inc(sem.lw, 16)
+    if we < 4:
+        g.sync.dma_start(T.ws[:, 512 * we:2048], T.w[:, 512 * we:2048]).then_inc(sem.lw, 16)
     for k in range(8):
         g.sync.dma_start(T.pls[16 * k:16 * k + 16, :], T.plt[:]).then_inc(sem.lp, 16)
-    V.wait_ge(sem.lt, 32)
-    for q in range(4):
-        for k, c in enumerate((1 - p, p)):
-            o_x = did(V.tensor_scalar(T.off[32 * q:32 * q + 32, :, 8 * k:8 * k + 8], T.trs[0:32, :, c, :], 4.0, 0.0, OP.mult, OP.max), "cv")
+    g.sync.wait_ge(sem.ct, 1)
+    g.sync.dma_start(T.vs[:], T.vv[:]).then_inc(sem.lv, 16)
     V.wait_ge(sem.lw0, 16)
-    q_w0 = quantise("wq", 0, 128, T.ws[:, 0:512])
+    q_w = q_w0 = quantise("wq", 0, 128 * we, T.ws[:, 0:512 * we])
+    V.wait_ge(sem.lt, R)
+    for j, job in enumerate(OPT["gather"]):
+        pa = p if JOBS[job][0] else 1 - p
+        pb = pa if JOBS[job][1] else 1 - pa
+        runs = [(0, 16, T.trs[0:R, :, pa, :, pb, :])]
+        if job == "A" and h != e:
+            runs = [(8 - 8 * f, 8, T.trs[0:R, f, pa, :, pb, :]) for f in (0, 1)]
+        for c, w, in_ in runs:
+            o_x = did(V.tensor_scalar(T.off[0:R, j, c:c + w], in_, 4.0, 0.0, OP.mult, OP.max), "cv")
+    if R < 128:
+        V.wait_ge(sem.cv, o_x)
+    for q in range(R, 128, R):
+        o_x = did(V.tensor_copy(T.off[q:q + R], T.off[0:R]), "cv")
 
-    chips = [at[1 - h, 1 - p, 0], at[h, 1 - p, 0], at[1 - h, p, 0], at[h, p, 0]]
-
-    def gather(s, j, t):
-        out, in_ = T.xg[:, 1024 * j + t:1024 * (j + 1):4], T.xs[:, t:2048].indirect(T.off[:, chips[j] // 2, :])
+    def gather(s, c, w, t):
+        out, in_ = T.xg[:, 4 * c + t:4 * (c + w):4], T.xs[:, t:2048].indirect(T.off[:, c // 256, c % 256 // 16:(c % 256 + w) // 16])
         if s == "cv":
             return did(V.tensor_copy(out, in_), "cv")
         return did(A.activation(out, in_, ACT.Copy), "cs")
@@ -223,62 +273,72 @@ def rank_program(g, core, T, topo):
     for q in (V, A):
         q.wait_ge(sem.lx, 16)
         q.wait_ge(sem.cv, o_x)
-    ka = [[gather("cs", j, t) for t in range(4 - SPLIT[j], 4)][-1] for j in range(4)]
+    pieces = []
+    for j, job in enumerate(OPT["gather"]):
+        pieces.append(("x" + job, 256 * j + 64 * (1 - e), 192) if job == "A" else ("x" + job, 256 * j, 256))
+    pieces.append((None, P["x0"]["A"] + 192 * e, 64))
+    split = OPT["split"]
+    ka = [[gather("cs", c, w, t) for t in range(4 - split[j], 4)][-1] for j, (st, c, w) in enumerate(pieces)]
     q_x = []
-    for j in range(4):
-        kv = [gather("cv", j, t) for t in range(4 - SPLIT[j])][-1]
+    for j, (st, c, w) in enumerate(pieces):
+        kv = [0] + [gather("cv", c, w, t) for t in range(4 - split[j])]
         V.wait_ge(sem.cs, ka[j])
-        V.wait_ge(sem.cv, kv)
-        if j < 3:
-            q_x.append(quantise("xq", 256 * j, 256, T.xg[:, 1024 * j:1024 * j + 1024]))
+        if kv[-1]:
+            V.wait_ge(sem.cv, kv[-1])
+        if st:
+            q_x.append(quantise("xq", c, w, T.xg[:, 4 * c:4 * (c + w)]))
         else:
-            quantise("xq", 768, 128, T.xg[:, 3072:3584])
-            q_x.append(quantise("nq", 192 * (1 - e), 128, T.xg[:, 3584:4096]))
-        if j == 0:
+            q_own = quantise("nq", 192 * (1 - e), 128, T.xg[:, 4 * c - 256 * e:4 * c - 256 * e + 512])
+        if j == OPT["wafter"] and we < 4:
             V.wait_ge(sem.lw, 16)
-            q_w = quantise("wq", 128, 384, T.ws[:, 512:2048])
-    g.sync.wait_ge(sem.cv, q_x[2])
-    g.sync.dma_start(T.vs[:], T.vv[:]).then_inc(sem.lv, 16)
+            q_w = quantise("wq", 128 * we, 512 - 128 * we, T.ws[:, 512 * we:2048])
 
     V.wait_ge(sem.lp, 128)
-    pt = lambda k: T.pt[:, k, :]
+    pt = lambda k, m=1: T.pt[:, k:k + m, :]
     up = did(V.tensor_scalar(pt(0), T.pls[:], 8.0, None, OP.mult), "cv")
     for k, b, m in ((1, 0, 64 + 15), (2, 4, 32), (3, 3, 16)):
         did(V.tensor_scalar(pt(k), T.pls[:], b, m, OP.arith_shift_right, OP.bitwise_and), "cv")
     V.wait_ge(sem.cv, up)
     for k, b, m in ((4, 0, 256 + 128), (5, 2, 512)):
-        kk = did(V.tensor_scalar(pt(k), pt(0), b, m, OP.arith_shift_right, OP.bitwise_and), "cv")
-    for step in (((6, 1, 2), (7, 3, 4)), ((8, 5, 6),), ((9, 7, 8),)):
-        V.wait_ge(sem.cv, kk)
-        for k, i, j in step:
-            kk = did(V.tensor_tensor(pt(k), pt(i), pt(j), OP.add), "cv")
-    V.wait_ge(sem.cv, kk)
-    did(V.tensor_copy(T.yo[:], pt(9)), "cv")
+        did(V.tensor_scalar(pt(k), pt(0), b, m, OP.arith_shift_right, OP.bitwise_and), "cv")
 
-    g.wait_ge(sem.cv, q_w0)
-    send("w0")
-    g.wait_ge(sem.cv, q_x[0])
-    send("x0c", "x0s")
-    g.wait_ge(sem.cv, q_w)
-    send("w1")
-    for j in (1, 2, 3):
+    if we:
+        g.wait_ge(sem.cv, q_w0)
+        send("w0")
+    for j, (st, c, w) in enumerate(pieces[:4]):
         g.wait_ge(sem.cv, q_x[j])
-        send("x%dc" % j, "x%ds" % j)
+        send(st + "c", st + "s")
+        if j == OPT["wafter"] and we < 4:
+            g.wait_ge(sem.cv, q_w)
+            send("w1")
 
-    X.wait_ge(sem.cv, q_x[3])
-    for k, (s, src, c0, order, H) in enumerate((("jn", "nq", 64 * e, near_order(rank), T.h0), ("jf", "fq", 0, range(4), T.h1))):
+    X.wait_ge(sem.cv, q_w)
+    for i, job in enumerate(OPT["rank"]):
+        k = "AC".index(job)
+        s, src, c0, order, H = (("jn", "nq", 64 * e, near_order(rank), T.h0), ("jf", "fq", 0, range(4), T.h1))[k]
+        if job == "A":
+            X.wait_ge(sem.cv, q_own)
         arrived(X, s)
-        first_stage(src, c0, order, H, 4 * k)
-        quantise("hq", 256 + 128 * k, 128, H[:, 2 - 2 * h:4 - 2 * h, :])
+        first_stage(src, c0, order, H)
+        q_o = quantise("hq", 256 + 128 * k, 128, H[:, 2 - 2 * h:4 - 2 * h, :])
         q_h = quantise("hq", 128 * k, 128, H[:, 2 * h:2 * h + 2, :])
-        g.wait_ge(sem.cv, q_h)
-        send("h%dc" % k, "h%ds" % k)
+        if (core, "t%sc" % job) in S:
+            g.wait_ge(sem.cv, q_o)
+            send("h%sc" % job, "h%ss" % job)
+            g.wait_ge(sem.cv, q_h)
+            send("t%sc" % job, "t%ss" % job)
+        else:
+            g.wait_ge(sem.cv, q_h)
+            send("h%sc" % job, "h%ss" % job)
     V.wait_ge(sem.lv, 16)
     q_v = did(V.quantize_mx(T.vq[:], T.vp[:], T.vs[:]), "cv")
+    for k, i, j, m in ((6, 1, 3, 2), (8, 6, 7, 1), (9, 8, 5, 1)):
+        kk = did(V.tensor_tensor(pt(k, m), pt(i, m), pt(j, m), OP.add), "cv")
+        V.wait_ge(sem.cv, kk)
+    did(V.tensor_copy(T.yo[:], pt(9)), "cv")
 
-    def second_stage(bank, src, c, w, s, where):
-        k = did(X.matmul_mx(T.ps[:, 512 * bank:512 * bank + w], T.vq[:], T.vp[:], T[src][:, c:c + w], T[PLANE[src]][:, c:c + w], True, True), "ct")
-        queue[s].wait_ge(sem.ct, k)
+    def second_stage(src, c, w, where):
+        bank, s = product(w, "vq", 0, src, c)
         for c0, w, a, ps in where:
             to = 512 * ps + 256 * par[a] + 128 * die[a] + 64 * hst[a]
             out, in_ = T.ys[:, to:to + w], T.ps[:, 512 * bank + c0:512 * bank + c0 + w]
@@ -286,30 +346,32 @@ def rank_program(g, core, T, topo):
                 k = did(V.tensor_copy(out, in_), "cv")
             else:
                 k = did(A.activation(out, in_, ACT.Copy), "cs")
-        return k
+        read.append((s, k))
 
     X.wait_ge(sem.cv, q_v)
-    X.wait_ge(sem.cs, n["cs"])
-    own = second_stage(0, "hq", 0, 256, "cs", [(64 * e, 64, rank, p), (128 + 64 * e, 64, rank, 1 - p)])
-    for k in range(4):
-        arrived(X, "y%d" % k)
-        ps = p if k in (0, 3) else 1 - p
-        if k % 2 == 0:
-            second_stage(2 * k + 1, "yq", 256 * k, 128, "cv", [(0, 128, at[0, p, 1 - e], ps)])
-            second_stage(2 * k + 2, "yq", 256 * k + 64, 128, "cs", [(64, 64, at[1 - h, p, e], ps)])
+    second_stage("hq", 0, 256, [(64 * e, 64, rank, p), (128 + 64 * e, 64, rank, 1 - p)])
+    for job in OPT["last"]:
+        arrived(X, "y" + job)
+        ps = p if job in "AD" else 1 - p
+        if job == "T":
+            calls = [(P["y0"]["A"] + 128, [(64 * k, 64, at[h, p, 1 - e], p ^ k) for k in (0, 1)])]
+        elif JOBS[job][1]:
+            calls = [(P["y0"][job], [(64 * d, 64, at[1 - h, p, d], ps) for d in (0, 1)])]
         else:
-            second_stage(2 * k + 1, "yq", 256 * k, 128, "cv", [(0, 128, at[0, 1 - p, 0], ps)])
-            if k == 3:
-                X.wait_ge(sem.cs, own)
-            second_stage((2 * k + 2) % 8, "yq", 256 * k + 128, 128, "cs", [(0, 128, at[0, 1 - p, 1], ps)])
+            calls = [(P["y0"][job] + 128 * d, [(0, 128, at[0, 1 - p, d], ps)]) for d in (0, 1)]
+        for c, where in calls:
+            second_stage("yq", c, 128, where)
     for q in (V, A):
         q.wait_ge(sem.cv, n["cv"])
         q.wait_ge(sem.cs, n["cs"])
-    kv = did(V.tensor_copy(T.yb[:, 0:256], T.ys[:].indirect(T.yo[:, 0:16])), "cv")
-    ks = did(A.activation(T.yb[:, 256:512], T.ys[:].indirect(T.yo[:, 16:32]), ACT.Copy), "cs")
-    g.sync.wait_ge(sem.cv, kv)
-    g.sync.dma_start(T.y[:, 0:256], T.yb[:, 0:256]).then_inc(sem.ly, 16)
-    A.wait_ge(sem.cs, ks)
-    A.dma_start(T.y[:, 256:512], T.yb[:, 256:512]).then_inc(sem.ly, 16)
-    g.wait_ge(sem.ly, 32)
+    w = 512 // OPT["stores"]
+    done = []
+    for k in range(OPT["stores"]):
+        out, in_ = T.yb[:, w * k:w * k + w], T.ys[:].indirect(T.yo[:, w * k // 16:w * (k + 1) // 16])
+        done.append(did(V.tensor_copy(out, in_), "cv") if k % 2 == 0 else did(A.activation(out, in_, ACT.Copy), "cs"))
+    for k in range(OPT["stores"]):
+        q = A if k == OPT["stores"] - 1 else g.sync
+        q.wait_ge(sem[("cv", "cs")[k % 2]], done[k])
+        q.dma_start(T.y[:, w * k:w * k + w], T.yb[:, w * k:w * k + w]).then_inc(sem.ly, 16)
+    g.wait_ge(sem.ly, 16 * OPT["stores"])
     finish()

from concourse.bass import DstId, RemoteDMATransfer
from concourse.mybir import dt, AluOpType, ActivationFunctionType

Q8 = "float8_e4m3fn_x4"
SCRATCH = {
    "trs": ("sbuf", [128, 2, 2, 4, 2, 2], "int32"),
    "off": ("sbuf", [128, 4, 16], "uint16"),
    "xs": ("sbuf", [128, 2048], "bfloat16"),
    "xg": ("sbuf", [128, 4096], "bfloat16"),
    "ws": ("sbuf", [128, 2048], "bfloat16"),
    "vs": ("sbuf", [128, 512], "bfloat16"),
    "xq": ("sbuf", [128, 1024], Q8), "xp": ("sbuf", [128, 1024], "uint8"),
    "wq": ("sbuf", [128, 512], Q8), "wp": ("sbuf", [128, 512], "uint8"),
    "vq": ("sbuf", [128, 128], Q8), "vp": ("sbuf", [128, 128], "uint8"),
    "rq": ("sbuf", [128, 256], Q8), "rp": ("sbuf", [128, 256], "uint8"),
    "nq": ("sbuf", [128, 320], Q8), "np": ("sbuf", [128, 320], "uint8"),
    "fq": ("sbuf", [128, 256], Q8), "fp": ("sbuf", [128, 256], "uint8"),
    "h0": ("sbuf", [128, 4, 256], "bfloat16"),
    "h1": ("sbuf", [128, 4, 256], "bfloat16"),
    "hq": ("sbuf", [128, 512], Q8), "hp": ("sbuf", [128, 512], "uint8"),
    "yq": ("sbuf", [128, 1024], Q8), "yp": ("sbuf", [128, 1024], "uint8"),
    "pls": ("sbuf", [128, 32], "int32"),
    "yo": ("sbuf", [128, 32], "uint16"),
    "pt": ("sbuf", [128, 10, 32], "int32"),
    "ys": ("sbuf", [128, 1024], "float32"),
    "yb": ("sbuf", [128, 512], "float32"),
    "ps": ("psum", [128, 4096], "float32"),
}
SEMAPHORES = ["lt", "lx", "lw0", "lw", "lv", "lp", "ly", "cv", "cs", "ct", "snd",
              "w0", "w1", "w2", "w3", "rC", "rD", "jn", "jf", "yA", "yB", "yC", "yD", "yT"]
PLANE = {"xq": "xp", "wq": "wp", "vq": "vp", "rq": "rp", "nq": "np", "fq": "fp", "hq": "hp", "yq": "yp"}
N, WORLD = 8, 256
JOBS = {"A": (True, True), "B": (True, False), "C": (False, True), "D": (False, False)}
OPT = dict(gather="DCBA", rank="AC", last="BATDC", two=1, tri=(0, 1, 0, 0), shape=((0, 0, 256), (1, 0, 256), (2, 0, 128), (2, 128, 128), (3, 0, 128), (3, 128, 128)), split=(2, 3, 2, 3, 4), w="m1", wafter=0, stores=4, via="host", tsplit="", dm=False, early=1, w0="swap",
           pool={"w0": "all", "w1": "all", "we": "lo", "wf": "all"})


def make_plan(T, topo):
    C = T.cores
    par = [0 if topo.chip(C[r]) == topo.chip(C[0]) or topo.same_plane(C[r], C[0]) else 1 for r in range(N)]
    die = [0 if topo.die(C[r]) == topo.die(C[0]) else 1 for r in range(N)]
    hst = [0 if topo.host(C[r]) == topo.host(C[0]) else 1 for r in range(N)]
    at = {(hst[r], par[r], die[r]): r for r in range(N)}
    assert all(at[h, p, d] == 4 * h + 2 * p + d for h, p, d in at)
    m1, m2, mate = [], [], []
    for r in range(N):
        far = [C[q] for q in range(N) if par[q] != par[r]][0]
        port = [c for c in topo.cores_of(C[r]) if topo.die(c) == topo.die(C[r]) and c != C[r] and topo.may_write(c, far)]
        m1.append(port[0])
        m2.append(port[1])
        mate.append([c for c in range(WORLD) if topo.mates(c, C[r]) and topo.die(c) == topo.die(C[r]) and topo.may_write(c, C[r])])
    dm = [m[0] for m in mate] if OPT["dm"] else m2
    S, relay = {}, {}
    x0 = {job: 256 * j for j, job in enumerate(OPT["gather"])}
    y0 = {job: 256 * j for j, job in enumerate("ABCD")}

    def slot(s, a):
        j = 2 * (hst[s] ^ hst[a]) + (die[s] ^ die[a])
        return 64 + 64 * j if die[a] else 192 - 64 * j

    for s in range(N):
        p, e, h = par[s], die[s], hst[s]
        me, twin = 64 * (2 * h + e), at[h, p, 1 - e]
        we = OPT["early"]
        tiles = [("wq", 128 * i, "wq", 128 * i, 128) for i in range(4)] + [("wp", 0, "wp", 0, 512)]
        early, rest = (tiles[:we], tiles[we:]) if we < 4 else (tiles, [])
        if we == 1:
            early = [("wq", 64 * i, "wq", 64 * i, 64) for i in (0, 1)]
        for parts, go, on, s0, s1, mode in ((early, "w0", "we", "w0", "w1", OPT["w0"]), (rest, "w1", "wf", "w2", "w3", OPT["w"])):
            if not parts:
                continue
            k = {"swap": len(parts) // 2, "m1": len(parts), "m2": 0, "both": 0}[mode]
            if mode == "both":
                S[C[s], go] = [(m,) + r + (s0,) for m in (m1[s], m2[s]) for r in parts]
                if OPT["dm"]:
                    S[m2[s], on] = [(dm[s],) + r + (s1,) for r in parts]
                continue
            S[C[s], go] = [((m1[s], m2[s])[i >= k],) + r + (s0,) for i, r in enumerate(parts)]
            if parts[:k]:
                S[m1[s], on] = [(dm[s],) + r + (s1,) for r in parts[:k]]
            if parts[k:]:
                S[m2[s], on] = [(c,) + r + (s1,) for c in (dm[s], m1[s]) if c != m2[s] for r in parts[k:]]
        if OPT["dm"]:
            S[C[s], "xD"] = [(dm[at[f, 1 - p, d]], "xq", x0["D"] + 128 * f + 64 * d, "fq", me, 64, "jf") for f in (0, 1) for d in (0, 1)]
            relay[m1[s]] = None
        for k, job, to in ((0, "C", C), (1, "D", m2))[:2 - OPT["dm"]]:
            k = (k, 0)[OPT["dm"]]
            S[C[s], "x" + job] = []
            ways = ((1 - h, mate[at[1 - h, 1 - p, e]][k * OPT["two"]]), (h, (m1, m2)[k or OPT["dm"]][s]))
            if OPT["via"] == "job":
                ways = [(f, mate[at[f, 1 - p, e]][h] if job == OPT["gather"][0] else (m1, m2)[f][s]) for f in (1 - h, h)]
            if OPT["via"] == "src" or (OPT["via"] == "half" and job != OPT["gather"][0]):
                ways = ((1 - h, (m2, m1)[k][s]), (h, (m1, m2)[k][s]))
            if OPT["via"] == "mate":
                ways = [(f, mate[at[f, 1 - p, e]][h]) for f in (1 - h, h)]
                relay[m1[s]] = relay[m2[s]] = None
            for f, via in ways:
                S[C[s], "x" + job].append((via, "xq", x0[job] + 128 * f, "rq", 128 * k, 128, "r" + job))
                S[via, "r" + job] = [(to[at[f, 1 - p, d]], "rq", 128 * k + 64 * d, "fq", me, 64, "jf") for d in (0, 1)]
                relay[via] = job
        near = [at[f, p, d] for f in (0, 1) for d in (0, 1)]
        S[C[s], "xB"] = [(m1[a], "xq", x0["B"] + 64 * j, "nq", slot(s, a), 64, "jn") for j, a in enumerate(near)]
        S[C[s], "xA"] = [(C[a], "xq", x0["A"] + 64 * j, "nq", slot(s, a), 64, "jn") for j, a in ((2 - 2 * e, at[1 - h, p, 0]), (3 - 2 * e, at[1 - h, p, 1]), (1 + e, twin))]
        for k, job in enumerate("AC"):
            S[C[s], "h" + job] = [(C[at[1 - h, p, d]], "hq", 256 + 128 * k + 64 * d, "yq", y0[job] + 64 * e, 64, "y" + job) for d in (0, 1)]
            S.setdefault((C[s], ("t" if job in OPT["tsplit"] else "h") + job), []).append(
                (C[twin], "hq", 128 * k + 64 * (1 - e), "yq", y0["A"] + 128 + 64 * k, 64, "yT"))
        for m, job in ((m1, "B"), (dm, "D")):
            S[m[s], "h"] = [(C[at[f, 1 - p, d]], "hq", 128 * f + 64 * d, "yq", y0[job] + 128 * e + 64 * h, 64, "y" + job) for f in (0, 1) for d in (0, 1)]
    calls = {}
    for (c, st), moves in S.items():
        if st[0] == "w":
            calls[c, st] = moves
        else:
            calls[c, st + "c"] = moves
            calls[c, st + "s"] = [(d, PLANE[sb], sc, PLANE[db], dc, w, k) for d, sb, sc, db, dc, w, k in moves]
    return dict(C=C, par=par, die=die, hst=hst, at=at, m1=m1, dm=dm, relay=relay, S=calls, x0=x0, y0=y0)


def engines_of(core, st, moves, topo, away):
    own = topo.cores_of(core)
    lo = topo.engines(core, away)
    every = topo.engines(core, [c for c in own if c != core][0])
    pool = {"lo": lo, "hi": [k for k in every if k not in lo], "all": every}[OPT["pool"].get(st[:2], "hi")]
    out = {}
    for js, ok in (([j for j, m in enumerate(moves) if m[0] not in own], lo), ([j for j, m in enumerate(moves) if m[0] in own], pool)):
        share = [1] * len(js)
        k = 0
        while js and sum(share) + share[k] <= len(ok):
            share[k] *= 2
            k = (k + 1) % len(js)
        for i, j in enumerate(js):
            out[j] = ok[sum(share[:i]):sum(share[:i + 1])]
    return [out[j] for j in range(len(moves))]


def rank_program(g, core, T, topo):
    P = make_plan(T, topo)
    S, C, par, die, hst, at = P["S"], P["C"], P["par"], P["die"], P["hst"], P["at"]
    rank = T.rank_of(core)
    if rank is None and core not in P["relay"]:
        return
    sem, V, A, X = T.sem, g.vector, g.scalar, g.tensor
    ACT, OP = ActivationFunctionType, AluOpType
    queue = {"cv": V, "cs": A}

    def engines(c, st):
        return engines_of(c, st, S[c, st], topo, [r for r in C if topo.same_plane(c, r)][0])

    due = {}
    for (c, st), moves in S.items():
        if any(m[0] == core for m in moves):
            for m, en in zip(moves, engines(c, st)):
                if m[0] == core:
                    due[m[6]] = due.get(m[6], 0) + len(en)
    n = {"cv": 0, "cs": 0, "ct": 0, "snd": 0}

    def did(ins, s):
        ins.then_inc(sem[s], 1)
        n[s] += 1
        return n[s]

    def arrived(q, s):
        if s in due:
            q.wait_ge(sem[s], due[s])

    def send(*calls):
        for st in calls:
            tr = []
            for (d, sb, sc, db, dc, w, s), e in zip(S[core, st], engines(core, st)):
                rid, pid = topo.addr(d, core)
                src, dst = T[sb][:, sc:sc + w], T[db][:, dc:dc + w]
                if sb in PLANE:
                    src, dst = src.bitcast(dt.uint8), dst.bitcast(dt.uint8)
                tr.append(RemoteDMATransfer(dst_ids=[DstId(rid=rid, pnc=pid)], dma_engine_mask=sum(1 << k for k in e),
                                            remote_sem=sem[s], srcs=[src], dsts=[dst]))
                n["snd"] += len(e)
            g.remote_dma_fused(tr, local_sem=sem.snd)

    def quantise(q, c, w, tile):
        return did(V.quantize_mx(T[q][:, c:c + w], T[PLANE[q]][:, c:c + w], tile), "cv")

    read = []

    def product(w, q, i, src, c):
        k = len(read)
        if k >= 8:
            X.wait_ge(sem[read[k - 8][0]], read[k - 8][1])
        kk = did(X.matmul_mx(T.ps[:, 512 * (k % 8):512 * (k % 8) + w], T[q][:, 128 * i:128 * i + 128], T[PLANE[q]][:, 128 * i:128 * i + 128],
                             T[src][:, c:c + w], T[PLANE[src]][:, c:c + w], True, True), "ct")
        s = ("cv", "cs")[k % 2]
        queue[s].wait_ge(sem.ct, kk)
        return k % 8, s

    def first_stage(src, c0, order, H):
        for i, u, w in OPT["shape"]:
            bank, s = product(w, "wq", i, src, c0 + u)
            for j in range(w // 64):
                c, in_ = 64 * order[u // 64 + j], T.ps[:, 512 * bank + 64 * j:512 * bank + 64 * j + 64]
                out = H[:, :, c + i:c + 64:4]
                if s == "cv":
                    did(V.tensor_scalar(out, in_, 0.0, 0.043, OP.max, OP.mult), "cv")
                else:
                    did(A.activation(out, in_, ACT.Relu, scale=0.043), "cs")
            read.append((s, n[s]))
        V.wait_ge(sem.cv, n["cv"])
        V.wait_ge(sem.cs, n["cs"])

    def near_order(a):
        order = [2 * (hst[a] ^ (j >> 1)) + (die[a] ^ (j & 1)) for j in range(4)]
        return order if die[a] else order[::-1]

    def finish():
        for s in ("cv", "cs", "ct", "snd"):
            if n[s]:
                g.wait_ge(sem[s], n[s])

    if rank is None:
        first, second = core in P["m1"], core in P["dm"]
        if (core, "we") in S:
            arrived(g, "w0"), send("we")
        steps = [("r" + job, ("r%sc" % job, "r%ss" % job)) for job in OPT["gather"]]
        steps.insert(OPT["wafter"] + 1, ("w2", ("wf",)))
        for s, calls in steps:
            if (core, calls[0]) in S:
                arrived(g, s), send(*calls)
        if first or second:
            for s in ("w0", "w1", "w2", "w3"):
                arrived(X, s)
            if first:
                a = P["m1"].index(core)
                arrived(X, "jn"), first_stage("nq", 64 * die[a], near_order(a), T.h0)
            else:
                arrived(X, "jf"), first_stage("fq", 0, range(4), T.h0)
            g.wait_ge(sem.cv, quantise("hq", 0, 256, T.h0[:]))
            send("hc", "hs")
        return finish()

    p, e, h = par[rank], die[rank], hst[rank]
    we, R = OPT["early"], 16 * len(OPT["tri"])
    g.scalar.dma_start(T.ws[:, 0:512 * we], T.w[:, 0:512 * we]).then_inc(sem.lw0, 16)
    for k, q in enumerate(OPT["tri"]):
        (g.sync, g.scalar)[q].dma_start(T.trs[16 * k:16 * k + 16], T.tri[:]).then_inc(sem.lt, 16)
    g.sync.dma_start(T.xs[:], T.x[:]).then_inc(sem.lx, 16)
    if we < 4:
        g.sync.dma_start(T.ws[:, 512 * we:2048], T.w[:, 512 * we:2048]).then_inc(sem.lw, 16)
    for k in range(8):
        g.sync.dma_start(T.pls[16 * k:16 * k + 16, :], T.plt[:]).then_inc(sem.lp, 16)
    g.sync.wait_ge(sem.ct, 1)
    g.sync.dma_start(T.vs[:], T.vv[:]).then_inc(sem.lv, 16)
    V.wait_ge(sem.lw0, 16)
    q_w = q_w0 = quantise("wq", 0, 128 * we, T.ws[:, 0:512 * we])
    V.wait_ge(sem.lt, R)
    for j, job in enumerate(OPT["gather"]):
        pa = p if JOBS[job][0] else 1 - p
        pb = pa if JOBS[job][1] else 1 - pa
        runs = [(0, 16, T.trs[0:R, :, pa, :, pb, :])]
        if job == "A" and h != e:
            runs = [(8 - 8 * f, 8, T.trs[0:R, f, pa, :, pb, :]) for f in (0, 1)]
        for c, w, in_ in runs:
            o_x = did(V.tensor_scalar(T.off[0:R, j, c:c + w], in_, 4.0, 0.0, OP.mult, OP.max), "cv")
    if R < 128:
        V.wait_ge(sem.cv, o_x)
    for q in range(R, 128, R):
        o_x = did(V.tensor_copy(T.off[q:q + R], T.off[0:R]), "cv")

    def gather(s, c, w, t):
        out, in_ = T.xg[:, 4 * c + t:4 * (c + w):4], T.xs[:, t:2048].indirect(T.off[:, c // 256, c % 256 // 16:(c % 256 + w) // 16])
        if s == "cv":
            return did(V.tensor_copy(out, in_), "cv")
        return did(A.activation(out, in_, ACT.Copy), "cs")

    for q in (V, A):
        q.wait_ge(sem.lx, 16)
        q.wait_ge(sem.cv, o_x)
    pieces = []
    for j, job in enumerate(OPT["gather"]):
        pieces.append(("x" + job, 256 * j + 64 * (1 - e), 192) if job == "A" else ("x" + job, 256 * j, 256))
    pieces.append((None, P["x0"]["A"] + 192 * e, 64))
    split = OPT["split"]
    ka = [[gather("cs", c, w, t) for t in range(4 - split[j], 4)][-1] for j, (st, c, w) in enumerate(pieces)]
    q_x = []
    for j, (st, c, w) in enumerate(pieces):
        kv = [0] + [gather("cv", c, w, t) for t in range(4 - split[j])]
        V.wait_ge(sem.cs, ka[j])
        if kv[-1]:
            V.wait_ge(sem.cv, kv[-1])
        if st:
            q_x.append(quantise("xq", c, w, T.xg[:, 4 * c:4 * (c + w)]))
        else:
            q_own = quantise("nq", 192 * (1 - e), 128, T.xg[:, 4 * c - 256 * e:4 * c - 256 * e + 512])
        if j == OPT["wafter"] and we < 4:
            V.wait_ge(sem.lw, 16)
            q_w = quantise("wq", 128 * we, 512 - 128 * we, T.ws[:, 512 * we:2048])

    V.wait_ge(sem.lp, 128)
    pt = lambda k, m=1: T.pt[:, k:k + m, :]
    up = did(V.tensor_scalar(pt(0), T.pls[:], 8.0, None, OP.mult), "cv")
    for k, b, m in ((1, 0, 64 + 15), (2, 4, 32), (3, 3, 16)):
        did(V.tensor_scalar(pt(k), T.pls[:], b, m, OP.arith_shift_right, OP.bitwise_and), "cv")
    V.wait_ge(sem.cv, up)
    for k, b, m in ((4, 0, 256 + 128), (5, 2, 512)):
        did(V.tensor_scalar(pt(k), pt(0), b, m, OP.arith_shift_right, OP.bitwise_and), "cv")

    if we:
        g.wait_ge(sem.cv, q_w0)
        send("w0")
    for j, (st, c, w) in enumerate(pieces[:4]):
        g.wait_ge(sem.cv, q_x[j])
        send(st + "c", st + "s")
        if j == OPT["wafter"] and we < 4:
            g.wait_ge(sem.cv, q_w)
            send("w1")

    X.wait_ge(sem.cv, q_w)
    for i, job in enumerate(OPT["rank"]):
        k = "AC".index(job)
        s, src, c0, order, H = (("jn", "nq", 64 * e, near_order(rank), T.h0), ("jf", "fq", 0, range(4), T.h1))[k]
        if job == "A":
            X.wait_ge(sem.cv, q_own)
        arrived(X, s)
        first_stage(src, c0, order, H)
        q_o = quantise("hq", 256 + 128 * k, 128, H[:, 2 - 2 * h:4 - 2 * h, :])
        q_h = quantise("hq", 128 * k, 128, H[:, 2 * h:2 * h + 2, :])
        if (core, "t%sc" % job) in S:
            g.wait_ge(sem.cv, q_o)
            send("h%sc" % job, "h%ss" % job)
            g.wait_ge(sem.cv, q_h)
            send("t%sc" % job, "t%ss" % job)
        else:
            g.wait_ge(sem.cv, q_h)
            send("h%sc" % job, "h%ss" % job)
    V.wait_ge(sem.lv, 16)
    q_v = did(V.quantize_mx(T.vq[:], T.vp[:], T.vs[:]), "cv")
    for k, i, j, m in ((6, 1, 3, 2), (8, 6, 7, 1), (9, 8, 5, 1)):
        kk = did(V.tensor_tensor(pt(k, m), pt(i, m), pt(j, m), OP.add), "cv")
        V.wait_ge(sem.cv, kk)
    did(V.tensor_copy(T.yo[:], pt(9)), "cv")

    def second_stage(src, c, w, where):
        bank, s = product(w, "vq", 0, src, c)
        for c0, w, a, ps in where:
            to = 512 * ps + 256 * par[a] + 128 * die[a] + 64 * hst[a]
            out, in_ = T.ys[:, to:to + w], T.ps[:, 512 * bank + c0:512 * bank + c0 + w]
            if s == "cv":
                k = did(V.tensor_copy(out, in_), "cv")
            else:
                k = did(A.activation(out, in_, ACT.Copy), "cs")
        read.append((s, k))

    X.wait_ge(sem.cv, q_v)
    second_stage("hq", 0, 256, [(64 * e, 64, rank, p), (128 + 64 * e, 64, rank, 1 - p)])
    for job in OPT["last"]:
        arrived(X, "y" + job)
        ps = p if job in "AD" else 1 - p
        if job == "T":
            calls = [(P["y0"]["A"] + 128, [(64 * k, 64, at[h, p, 1 - e], p ^ k) for k in (0, 1)])]
        elif JOBS[job][1]:
            calls = [(P["y0"][job], [(64 * d, 64, at[1 - h, p, d], ps) for d in (0, 1)])]
        else:
            calls = [(P["y0"][job] + 128 * d, [(0, 128, at[0, 1 - p, d], ps)]) for d in (0, 1)]
        for c, where in calls:
            second_stage("yq", c, 128, where)
    for q in (V, A):
        q.wait_ge(sem.cv, n["cv"])
        q.wait_ge(sem.cs, n["cs"])
    w = 512 // OPT["stores"]
    done = []
    for k in range(OPT["stores"]):
        out, in_ = T.yb[:, w * k:w * k + w], T.ys[:].indirect(T.yo[:, w * k // 16:w * (k + 1) // 16])
        done.append(did(V.tensor_copy(out, in_), "cv") if k % 2 == 0 else did(A.activation(out, in_, ACT.Copy), "cs"))
    for k in range(OPT["stores"]):
        q = A if k == OPT["stores"] - 1 else g.sync
        q.wait_ge(sem[("cv", "cs")[k % 2]], done[k])
        q.dma_start(T.y[:, w * k:w * k + w], T.yb[:, w * k:w * k + w]).then_inc(sem.ly, 16)
    g.wait_ge(sem.ly, 16 * OPT["stores"])
    finish()
